import numpy as np, ml_dtypes
CORES = [10,34,74,98]
N = 4
import mx_ref
BF = ml_dtypes.bfloat16
def gcols(t, e):
    v = np.concatenate([t.reshape(8, 16, -1, 4), np.zeros((8, 16, 1, 4), BF)], axis=2)
    return np.ascontiguousarray(np.stack([v[g][:, e[g]] for g in range(8)])).reshape(128, -1)
def tile(rs):
    return np.stack(rs, axis=2).reshape(128, -1).astype(BF)
def cut(t, i, w=512):
    return t[:, w * i:w * i + w]
def pick(q, e):
    c = np.concatenate([q[0].reshape(128, -1, 4), np.zeros((128, 1, 4), np.uint8)], axis=1); s = np.concatenate([q[1], np.ones((16, 1), np.uint8)], axis=1)
    return (np.ascontiguousarray(c[:, e].reshape(128, -1)), np.ascontiguousarray(s[:, e]))
def join(*qs):
    return (np.concatenate([q[0] for q in qs], axis=1), np.concatenate([q[1] for q in qs], axis=1))
def put(q, e, v):
    c, s = q[0].reshape(128, -1, 4).copy(), q[1].copy(); c[:, e] = v[0].reshape(128, -1, 4); s[:, e] = v[1]
    return (c.reshape(128, -1), s)
def pk(c, s):
    return (np.ascontiguousarray(c), mx_ref.live(s))
def emit(q):
    return q[0], q[1]
def packed(v, rng):
    q = [mx_ref.quantize(np.ascontiguousarray(v[r])) for r in range(N)]
    return np.stack([a for a, b in q]), np.stack([mx_ref.plane(b, rng) for a, b in q])
def f(rng, *shape):
    return mx_ref.flush((rng.standard_normal(shape, dtype=np.float32) * np.exp2(rng.integers(-2, 3, shape[:-1] + (1,)))).astype(BF))
def wide(rng, *shape, cols=0):
    v = rng.standard_normal(shape, dtype=np.float32) * np.exp2(rng.integers(-12, 13, shape)).astype(np.float32)
    if cols: v *= np.repeat(np.exp2(rng.integers(-cols, cols + 1, shape[:-2] + (1, shape[-1] // 4))) * (rng.random(shape[:-2] + (1, shape[-1] // 4)) > 0.0625), 4, axis=-1).astype(np.float32)
    return mx_ref.flush(v.astype(BF))
C, R = 320, 3
H = C // 2
STEP = [1, 2, 1]
def keep(t, gs):
    v = np.zeros((8, 16, t.shape[1]), BF)
    v[gs] = t.reshape(8, 16, -1)[gs]
    return v.reshape(128, -1)
def grams(a, b):
    n = a.shape[1] // 4
    qa = mx_ref.quantize(np.concatenate([keep(a, [m, m + 4]) for m in range(4)], axis=1))
    qb = mx_ref.quantize(np.concatenate([keep(b, [0, 1, 2, 3]), keep(b, [4, 5, 6, 7])], axis=1))
    z = np.zeros((8, n), np.float32)
    j = np.arange(32)
    for k in range(n // 32):
        e = 32 * k + j
        p = mx_ref.matmul(pick(qa, np.concatenate([e + n * m for m in range(4)])), pick(qb, np.concatenate([e, e + n])))
        for g in range(8): z[g, e] = p[32 * (g % 4) + j, 32 * (g // 4) + j]
    return z + np.float32(0.0)
def over(v):
    return np.repeat(np.repeat(v, 16, axis=0), 4, axis=1)
def big(v):
    v = v.astype(np.float32)
    v[np.abs(v) < np.float32(2.0 ** -16)] = 0
    return v.astype(BF)
def common(w, rng):
    c, p = packed(np.stack([w] * N), rng)
    return {"wc": c, "ws": p}
def weights(rng):
    return common(big(f(rng, 128, 2048)), rng)
def still(rng):
    w = np.zeros((128, 4, 128, 4), np.float32)
    i = np.arange(128)
    for b in range(4): w[i, b, i, b] = 32
    return common(w.reshape(128, 2048).astype(BF), rng)
def numbers_of(rng):
    return {"x": big(f(rng, N, 128, 4 * C)), "v": np.array(f(rng, N, 128, 512))}
def setup_inputs(rng):
    return {**numbers_of(rng), **weights(rng)}
def setup_inputs_ties(rng):
    d = numbers_of(rng)
    x = d["x"].reshape(N, 128, C, 4)
    o = rng.permutation(N)
    for r in range(N):
        k = np.zeros(C, int) if o[r] == 0 else rng.permutation(C) % 3
        a = x[r][:, :3].astype(np.float32)
        a[:, 2] = 0
        z = rng.choice([-1.0, 1.0], (128, 6, 4)).astype(np.float32)
        z[:, 5] = -z[:, 0]
        x[r] = (a[:, k] * z[:, rng.integers(0, 6, C)]).astype(BF)
        if o[r] == 1: x[r] = 0
    return {"x": x.reshape(N, 128, 4 * C), "v": d["v"], **weights(rng)}
def setup_inputs_near(rng):
    main = np.array([[0.75, 0.5, 0.25, 0.25, 0.25, 0, 0, 0], [0.25, 0.5, 0.5, 0.5, 0.25, 0.25, 0.25, 0], [0, 1, 0, 0, 0, 0, 0, 0]])
    size = np.where(rng.permutation(N) < N // 2, 2.0 ** -16, 1.0)
    x = np.zeros((N, 8, 16, C, 4))
    i = np.arange(H)
    s = 3 * i // 2
    tiny = 2.0 ** -11
    def fine(s):
        k = (s[:, None] >> np.array([0, 2, 4, 6])) & 3
        return (np.arange(4) < k[:, :, None]) * np.exp2(np.arange(4) - 11.0)[:, None]
    for r in range(N):
        for g in range(8):
            e = rng.permutation(C).reshape(H, 2)
            kind = np.where(i % 2 == 0, rng.integers(0, 2, H), rng.integers(0, 3, H))
            kind[:2] = (r + g) % 2, 2
            top, low = rng.choice([-1.0, 1.0], (2, H))
            z = np.zeros((C, 16, 4))
            z[e[:, 0], 0, 0] = 1
            z[e[:, 0], 8:12] = fine(s)
            z[e[:, 1], :8, 0] = top[:, None] * main[kind]
            z[e[:, 1], 8:12] = (top * low)[:, None, None] * fine(s + (kind == 2))
            for j in (H - 2, H - 1):
                z[e[j]] = 0
                z[e[j, 0], 0, 0] = 2
                z[e[j, 1], :8, 0] = 2 * main[0]
                z[e[j, 0], 8, :2] = tiny
                if j == H - 2:
                    z[e[j, 1], 8, 1:3] = tiny
                else:
                    z[e[j, 1], 8, 2:] = tiny
                    z[e[j], 9, 0] = 2 * tiny
                z[e[j, 1]] *= top[j]
            x[r, g] = z.transpose(1, 0, 2) * size[r]
    return {"x": x.astype(np.float32).reshape(N, 128, 4 * C).astype(BF), "v": np.array(f(rng, N, 128, 512)), **still(rng)}
def setup_inputs_huge(rng):
    o = rng.permutation(N)
    low = np.where(o == 0, 0.98, 0.8)[:, None, None, None, None]
    x = 2.0 ** 30 * (low + (1 - low) * rng.random((N, 8, 16, C, 4)))
    x[o == 0, :, ::8, :, 0] = 2.0 ** 30
    c = rng.choice([-1.0, 1.0], (N, 8, 1, C, 1))
    c[o % 2 == 1] = 1
    c[o % 2 == 0, :, :, ::3] = -1
    return {"x": (x * c).astype(np.float32).reshape(N, 128, 4 * C).astype(BF), "v": np.array(f(rng, N, 128, 512)), **still(rng)}
def setup_inputs_lean(rng):
    h = np.array([0.25, 0.5, 1.0, 2.0])[rng.integers(0, 4, (N, 1, C, 1))]
    o = rng.permutation(N)
    h[o == 0] = 0.125
    h[o == 1] = 4
    c = rng.choice([-1.0, 1.0], (N, 1, C, 1))
    a = rng.choice([-1.0, 1.0], (N, 128, 1, 4)) * (0.5 + rng.random((N, 128, 1, 4)))
    x = c * (a + h * rng.standard_normal((N, 128, C, 4)))
    return {"x": big(x.reshape(N, 128, 4 * C)), "v": np.array(f(rng, N, 128, 512)), **weights(rng)}
def setup_inputs_spread(rng):
    d = setup_inputs(rng)
    d["x"] = big(wide(rng, N, 128, 4 * C, cols=6))
    return d
def check_inputs(d):
    b = []
    for k in ("x", "v"):
        a = np.abs(d[k].astype(np.float32))
        if not (np.isfinite(a).all() and ((a == 0) | (a >= 2.0 ** -30) & (a <= 2.0 ** 30)).all()): b.append("a value of " + k)
    if ((d["wc"] & 127) == 127).any(): b.append("a code of wc")
    if (d["wc"] != d["wc"][:1]).any(): b.append("wc differs between ranks")
    s = [mx_ref.live(p) for p in d["ws"]]
    if any((p != s[0]).any() for p in s): b.append("ws differs between ranks")
    return b
def reference(x, v, wc, ws):
    w = pk(wc[0], ws[0])
    now = np.concatenate([x[r] for r in range(N)], axis=1)
    for t in range(R):
        d = grams(now, now)
        o = np.argsort(d.reshape(8, N, C), axis=2, kind="stable")
        at = o + C * np.arange(N)[:, None]
        even, odd = at[:, :, ::2].reshape(8, -1), at[:, :, 1::2].reshape(8, -1)
        a, b = gcols(now, even), gcols(now, odd)
        da = np.take_along_axis(d, even, axis=1)
        n = grams(a, b)
        c = np.where(np.abs(n) >= np.float32(0.75) * da, np.float32(1.0), np.where(np.abs(n) >= np.float32(0.25) * da, np.float32(0.5), np.float32(0.0))) * np.sign(n)
        left = (b.astype(np.float32) - over(c) * a.astype(np.float32)).astype(BF)
        swap = over(grams(left, left) < da)
        stay, go = np.where(swap, left, a), np.where(swap, a, left)
        q = mx_ref.quantize(np.ascontiguousarray(go))
        came = tile([mx_ref.matmul(pick(w, np.arange(128 * k, 128 * k + 128)), q) * np.float32(0.03125) for k in range(4)])
        now = np.concatenate([z for r in range(N) for z in (cut(stay, r, 4 * H), cut(came, (r - STEP[t]) % N, 4 * H))], axis=1)
    y, ol = np.zeros((N, 128, C), np.float32), np.zeros((N, 8, C), np.float32)
    oc, osc = np.zeros((N, 128, 4 * C), np.uint8), np.zeros((N, 16, C), np.uint8)
    for r in range(N):
        q = mx_ref.quantize(np.ascontiguousarray(cut(now, r, 4 * C)))
        y[r] = mx_ref.matmul(mx_ref.quantize(v[r]), q)
        ol[r] = o[:, r]
        oc[r], osc[r] = emit(q)
    return {"y": y, "ol": ol, "oc": oc, "osc": osc}

@@ -1,0 +1,529 @@
+from concourse.mybir import dt, AluOpType, ActivationFunctionType
+
+F, B, U16, I32, C4, U8 = "float32", "bfloat16", "uint16", "int32", "float8_e4m3fn_x4", "uint8"
+STEP = [1, 2, 1]
+W = 306
+NS = 12
+NS0 = 10
+NSS = 3
+NLATE = 1
+KV = (0,)
+PLAN_X = "q so0 so1 so2 so3 ve0 ve1 ve2 ve3"
+PLAN_K = "ve0 vo0 ve1 vo1 ve2 so2 so3 q ve3"
+PLAN_N = "ve2 so0 so1 so2 q ve0 ve1 ve3 vo3"
+PLAN_E = "so0 se0 so1 se1 so2 so3 q ve2 ve3"
+TINY = 2.0 ** -100
+BELOW = 1.0 - 2.0 ** -24
+FAR = -1.0e25
+
+
+def _sb(n, d):
+    return ("sbuf", [128, n], d)
+
+
+SCRATCH = {
+    "X": _sb(1296, B), "XP": _sb(1280, B), "G": _sb(1280, B), "AR": _sb(1280, B), "MV": _sb(1280, B), "M": _sb(640, B), "VT": _sb(512, B),
+    "QU": _sb(324, C4), "SU": _sb(324, U8), "QS": _sb(640, C4), "SS": _sb(640, U8), "QV": _sb(320, C4), "SV": _sb(320, U8),
+    "WC": _sb(512, C4), "WS": _sb(512, U8), "QW": _sb(128, C4), "SW": _sb(128, U8), "QF": _sb(320, C4), "SF": _sb(320, U8),
+    "Z": _sb(320, F), "ZM": _sb(160, F), "ZS": _sb(160, F), "EB": _sb(352, F), "U": _sb(672, F), "U2": _sb(320, F), "GC": _sb(32, F),
+    "Y": _sb(160, F), "DC": _sb(160, B), "DG": _sb(320, B), "CB": _sb(12 * 304, B), "SO": _sb(12 * 152, B),
+    "SB": _sb(14 * W, F), "SB2": _sb(10 * 144, F), "ACC": _sb(16, F), "OFFS": _sb(20, U16), "OR": _sb(352, B), "TT": _sb(672, B),
+    "OG": _sb(32, U16), "DS": _sb(320, F), "TD": _sb(160, F), "DA": _sb(160, F), "TH": _sb(48, F),
+    "CMP": _sb(48, F), "CS": _sb(48, F), "EC": _sb(160, B), "D0": _sb(320, B), "SD": _sb(160, B), "ST": _sb(160, B),
+    "PM": _sb(160, B), "PT": _sb(160, B), "OM": _sb(64, U16), "OS": _sb(64, U16),
+    "YO": _sb(320, F), "OLF": _sb(320, F),
+    "PI": _sb(8, I32), "COL": _sb(24, F), "MK": _sb(2, B), "J40": _sb(40, F), "JM": _sb(40, F), "JF": _sb(40, F), "J2": _sb(40, F), "LST": _sb(224, U16),
+    "RS16": _sb(160, B), "ONEB": _sb(160, B), "RS4": _sb(48, B), "FT0": _sb(160, F), "FT1": _sb(160, F), "FT": _sb(160, F),
+    "M16": _sb(160, F), "NEG0": _sb(160, F), "NEG": _sb(160, F), "LA": _sb(160, F), "LB": _sb(160, B), "LB2": _sb(160, B), "LM": _sb(160, B), "LS": _sb(160, B),
+    "IO": _sb(320, B), "KI": _sb(48, F), "KK": _sb(8, F), "LT": _sb(4, F),
+    "PS": ("psum", [128, 4096], F),
+}
+for _r in range(3):
+    SCRATCH["QM%d" % _r] = _sb(160, C4)
+    SCRATCH["SM%d" % _r] = _sb(160, U8)
+    SCRATCH["LC%d" % _r] = _sb(160, C4)
+    SCRATCH["LS%d" % _r] = _sb(160, U8)
+NDMA = 24
+SEMAPHORES = ["cv", "cs", "cp", "cg", "sent", "arr0", "arr1", "arr2"] + ["d%d" % _i for _i in range(NDMA)]
+
+L_PS, L_PK, L_PA, L_PR = 0, 40, 80, 120
+L_END, L_EX16, L_LC, L_X = 160, 170, 180, 190
+L_N, L_3R, L_3G = 200, 204, 206
+C16, CH, CU, C32, C4Q, CE, CNE, CX16, C64, C2X, CT4, CT5 = 1, 2, 3, 4, 5, 6, 7, 8, 9, 10, 11, 12
+
+
+def rank_program(g, core, T, topo):
+    rank = T.rank_of(core)
+    if rank is None:
+        return
+    A = AluOpType
+    ACT = ActivationFunctionType
+    eng = {"v": g.vector, "s": g.scalar, "p": g.tensor, "g": g, "y": g.sync}
+    sem = {"v": "cv", "s": "cs", "p": "cp", "g": "cg"}
+    count = {"v": 0, "s": 0, "p": 0, "g": 0}
+    known = {k: {} for k in eng}
+    hist = {}
+    ndma = [0]
+    bank = [0]
+
+    def R(name, a=0, b=None, s=1):
+        n = SCRATCH[name][1][1]
+        return (name, a, n if b is None else min(b, n), s)
+
+    def ap(r):
+        if r[3] == 1:
+            return T[r[0]][:, r[1]:r[2]]
+        return T[r[0]][:, r[1]:r[2]:r[3]]
+
+    def wait(q, tok):
+        if known[q].get(tok[0], 0) < tok[1]:
+            eng[q].wait_ge(T.sem[tok[0]], tok[1])
+            for k, val in tok[2].items():
+                if known[q].get(k, 0) < val:
+                    known[q][k] = val
+
+    def emit(q, fn, reads, writes, dma=False):
+        acc = []
+        for r in reads:
+            acc.append((r, r[0] == "PS"))
+        for r in writes:
+            acc.append((r, True))
+        need = {}
+        sets = []
+        for r, wr in acc:
+            if r[0] == "PS":
+                s = frozenset([r[1] // 512])
+            else:
+                s = frozenset(range(r[1], r[2], r[3]))
+            sets.append((r[0], s, wr))
+            for s2, wr2, tok in hist.get(r[0], []):
+                if (wr or wr2) and known[q].get(tok[0], 0) < tok[1] and not s.isdisjoint(s2):
+                    if tok[0] not in need or need[tok[0]][1] < tok[1]:
+                        need[tok[0]] = tok
+        for tok in need.values():
+            wait(q, tok)
+        if q == "g" and count["g"] > known["g"].get("cg", 0):
+            wait("g", ("cg", count["g"], {"cg": count["g"]}))
+        ins = fn(eng[q])
+        clock = dict(known[q])
+        if dma:
+            name = "d%d" % ndma[0]
+            ndma[0] += 1
+            ins.then_inc(T.sem[name], 16)
+            clock[name] = 16
+            tok = (name, 16, clock)
+        else:
+            count[q] += 1
+            ins.then_inc(T.sem[sem[q]], 1)
+            clock[sem[q]] = count[q]
+            tok = (sem[q], count[q], clock)
+        for name, s, wr in sets:
+            h = hist.setdefault(name, [])
+            if wr:
+                h[:] = [e for e in h if not e[0] <= s]
+            h.append((s, wr, tok))
+        return tok
+
+    def opnd(x):
+        if len(x) == 2:
+            return ap(x[0]).indirect(ap(x[1])), [x[0], x[1]]
+        return ap(x), [x]
+
+    def scal(x):
+        if isinstance(x, tuple):
+            return ap(x), [x]
+        return x, []
+
+    def col(c):
+        return R("COL", c, c + 1)
+
+    def lst(c, n):
+        return R("LST", c, c + n)
+
+    def ts(out, in0, s1, op0, s2=None, op1=None):
+        i, rd = opnd(in0)
+        a1, r1 = scal(s1)
+        a2, r2 = scal(s2)
+        if op1 is None:
+            return emit("v", lambda e: e.tensor_scalar(ap(out), i, a1, None, op0), rd + r1, [out])
+        return emit("v", lambda e: e.tensor_scalar(ap(out), i, a1, a2, op0, op1), rd + r1 + r2, [out])
+
+    def tt(out, in0, in1, op):
+        i, rd = opnd(in0)
+        return emit("v", lambda e: e.tensor_tensor(ap(out), i, ap(in1), op), rd + [in1], [out])
+
+    def cp(out, in_):
+        i, rd = opnd(in_)
+        return emit("v", lambda e: e.tensor_copy(ap(out), i), rd, [out])
+
+    def scan(out, d0, d1, init, op0, op1):
+        a, r = scal(init)
+        return emit("v", lambda e: e.tensor_tensor_scan(ap(out), ap(d0), ap(d1), a, op0, op1), [d0, d1] + r, [out])
+
+    def tr(out, in_):
+        return emit("v", lambda e: e.transpose(ap(out), ap(in_)), [in_], [out])
+
+    def mset(out, val):
+        return emit("v", lambda e: e.memset(ap(out), val), [], [out])
+
+    def act(out, in_, func, bias=None, scale=None, accum=None):
+        i, rd = opnd(in_)
+        kw = {}
+        wr = [out]
+        if bias is not None:
+            kw["bias"], r = scal(bias)
+            rd = rd + r
+        if scale is not None:
+            kw["scale"], r = scal(scale)
+            rd = rd + r
+        if accum is not None:
+            kw["accum_out"] = ap(accum)
+            wr = wr + [accum]
+        return emit("s", lambda e: e.activation(ap(out), i, func, **kw), rd, wr)
+
+    def gat(q, out, win, off):
+        if q == "v":
+            return cp(out, (win, off))
+        return act(out, (win, off), ACT.Copy)
+
+    def quant(qc, qs, a, n, tile):
+        oc, os_ = R(qc, a, a + n), R(qs, a, a + n)
+        return emit("v", lambda e: e.quantize_mx(ap(oc), ap(os_), ap(tile)), [tile], [oc, os_])
+
+    def mm(bk, n, lc, ls, la, rc, rs, ra):
+        o = R("PS", 512 * bk, 512 * bk + n)
+        rr = [R(lc, la, la + 128), R(ls, la, la + 128), R(rc, ra, ra + n), R(rs, ra, ra + n)]
+        return emit("p", lambda e: e.matmul_mx(ap(o), ap(rr[0]), ap(rr[1]), ap(rr[2]), ap(rr[3]), True, True), rr, [o])
+
+    def nextbank():
+        bank[0] = (bank[0] + 1) % 8
+        return bank[0]
+
+    def iota(out, pat, base, cm=0):
+        o = ap(out)
+        if SCRATCH[out[0]][2] == I32:
+            return emit("g", lambda e: e.iota(o, pat, base, cm), [], [out])
+        return emit("g", lambda e: e.iota(o, pat, base, cm, allow_small_or_imprecise_dtypes=True), [], [out])
+
+    def asel(out, in_, pat, op, fill, base, cm, quarter=None):
+        if quarter is None:
+            o, i = ap(out), ap(in_)
+        else:
+            o = T[out[0]][32 * quarter:32 * quarter + 32, out[1]:out[2]]
+            i = T[in_[0]][32 * quarter:32 * quarter + 32, in_[1]:in_[2]]
+        return emit("g", lambda e: e.affine_select(o, i, pat, op, fill, base, cm), [in_], [out])
+
+    def dma(q, out, in_, reads, writes):
+        return emit(q, lambda e: e.dma_start(out, in_), reads, writes, dma=True)
+
+    dma("y", T.X[:, 16:656], T.x[:, 0:640], [], [R("X", 16, 656)])
+    dma("y", T.X[:, 656:1296], T.x[:, 640:1280], [], [R("X", 656, 1296)])
+    dma("y", T.WC[:].bitcast(dt.uint8), T.wc[:], [], [R("WC")])
+    dma("y", T.WS[:], T.ws[:], [], [R("WS")])
+    dma("y", T.VT[:], T.v[:], [], [R("VT")])
+
+    p16 = [[0, 10], [1, 16]]
+    iota(R("PI", 0, 1), [[0, 1]], 0, 1)
+    iota(R("J40"), [[32, 5], [0, 4], [16, 2]], 0)
+    mset(R("X", 0, 16), 0.0)
+    mset(R("ONEB"), 1.0)
+    mset(R("U", 16, 208), 0.0)
+    for a in range(4):
+        asel(R("JM"), R("J40"), [[0, 5], [1, 4], [0, 2]], A.is_equal, -1000.0, -a, 0, quarter=a)
+    iota(R("KI", 30, 40), [[64, 5], [1, 2]], 0)
+    iota(R("FT0"), p16, 0)
+    iota(R("KI", 0, 10), [[16, 10]], 15)
+    iota(R("KI", 10, 20), [[1, 10]], 0)
+    iota(R("KI", 20, 30), [[4, 10]], 3)
+    asel(R("RS16"), R("ONEB"), p16, A.not_equal, 0.0, 0, 0)
+    iota(R("KK", 0, 2), [[256, 2]], 0)
+    iota(R("KK", 4, 8), [[4, 4]], 0)
+    iota(R("LA"), [[32, 10], [0, 16]], -159)
+    p0 = R("PI", 0, 1)
+    ts(R("PI", C16, C16 + 1), p0, 15, A.bitwise_and)
+    ts(R("PI", CH, CH + 1), p0, 4, A.logical_shift_right, 1, A.bitwise_and)
+    ts(R("PI", CU, CU + 1), p0, 1, A.bitwise_and)
+    ts(R("PI", C32, C32 + 1), p0, 31, A.bitwise_and)
+    ts(R("PI", C4Q, C4Q + 1), p0, 2, A.logical_shift_right, 3, A.bitwise_and)
+    mset(R("OR"), 0.0)
+    cp(R("COL", 1, 6), R("PI", 1, 6))
+    mset(R("D0"), 0.0)
+    ts(R("MK", 0, 1), col(CH), -1.0, A.mult, 1.0, A.add)
+    tt(col(CNE), col(CU), col(CH), A.not_equal)
+    ts(col(CX16), col(C16), 16.0, A.mult)
+    ts(col(C64), col(C32), 2.0, A.mult)
+    ts(col(C2X), col(C16), 2.0, A.mult)
+    cp(R("MK", 1, 2), col(CH))
+    ts(col(CE), col(CH), -1.0, A.mult, 1.0, A.add)
+    ts(col(CT5), col(CNE), 176.0, A.mult, col(CX16), A.add)
+    ts(col(CT4), col(CNE), 336.0, A.mult, col(CX16), A.add)
+    mset(R("TH"), 0.0)
+    ts(R("JF"), R("JM"), col(C16), A.add)
+    ts(lst(L_3R, 1), col(CT5), 351.0, A.min)
+    ts(lst(L_PS, 40), R("JF"), 4.0, A.add, 0.0, A.max)
+    ts(lst(L_PK, 40), R("JF"), 164.0, A.add, 0.0, A.max)
+    act(R("J2"), R("JF"), ACT.Copy, scale=2.0)
+    ts(lst(L_X, 10), R("KI", 30, 40), col(C64), A.add)
+    ts(lst(L_PA, 40), R("J2"), 4.0, A.add, 0.0, A.max)
+    ts(lst(L_PR, 40), R("J2"), 5.0, A.add, 0.0, A.max)
+
+    def setup2():
+        ts(R("M16"), R("FT0"), col(C16), A.is_equal)
+        cp(lst(L_END, 30), R("KI", 0, 30))
+        ts(R("FT1"), R("FT0"), col(C16), A.is_ge, -2.0 ** -24, A.mult)
+        act(R("FT"), R("FT1"), ACT.Identity, bias=1.0)
+
+    def setup3():
+        ts(R("LT"), R("KK", 4, 8), col(C4Q), A.add, 16.0, A.mult)
+        ts(lst(L_3G, 2), R("KK", 0, 2), col(CT4), A.add, 671.0, A.min)
+        ts(lst(L_N, 4), R("LT"), 15.0, A.add, 159.0, A.min)
+
+    def setup4():
+        act(R("NEG0"), R("M16"), ACT.Identity, bias=FAR, scale=-FAR)
+        act(R("LB"), R("LA"), ACT.Identity, bias=col(C2X))
+        act(R("NEG"), R("NEG0"), ACT.Identity, bias=-TINY)
+        act(R("LB2"), R("LB"), ACT.Identity, bias=-1.0)
+        iota(R("IO"), [[1, 320]], -160)
+        asel(R("RS4"), R("ONEB", 0, 48), [[0, 12], [1, 4]], A.not_equal, 0.0, 0, 0)
+        asel(R("LM"), R("LB"), p16, A.is_equal, -1000.0, 0, 0)
+        asel(R("LS"), R("LB2"), p16, A.is_equal, -1000.0, 0, 0)
+
+    def gram(src, tile, qa, qn, plist, e0, step, plan, smid=None, smid2=None, vmid=None):
+        for what in plan.split():
+            if what == "q":
+                quant("QU", "SU", qa, qn, tile)
+                continue
+            h, t = "eo".index(what[1]), int(what[2])
+            o, i = R("MV", 4 * h + t, 1280, 8), R(src, e0 + t, e0 + 160 * step, step)
+            if what[0] == "s":
+                act(o, i, ACT.Copy, scale=col(CH if h else CE))
+            else:
+                ts(o, i, R("MK", h, h + 1), A.mult)
+        quant("QV", "SV", 0, 320, R("MV"))
+        banks = []
+        for lo, hi in ((0, 3), (3, 5)):
+            off = lst(plist + 8 * lo, 8 * (hi - lo))
+            oc, os_ = R("QS", 128 * lo, 128 * hi), R("SS", 128 * lo, 128 * hi)
+            emit("s", lambda e: e.activation(ap(os_), T.SU[:, 0:324].indirect(ap(off)), ACT.Copy), [R("SU"), off], [os_])
+            emit("v", lambda e: e.tensor_copy(ap(oc).bitcast(dt.uint32), T.QU[:, 0:324].bitcast(dt.uint32).indirect(ap(off))), [R("QU"), off], [oc])
+            for b in range(lo, hi):
+                bk = nextbank()
+                banks.append(bk)
+                mm(bk, 128, "QS", "SS", 128 * b, "QV", "SV", min(64 * b, 192))
+            if lo == 0 and smid is not None:
+                smid()
+        if smid2 is not None:
+            smid2()
+        for b in range(5):
+            o = 512 * banks[b] + (64 if b == 4 else 0)
+            act(R("Z", 64 * b, 64 * b + 64), R("PS", o, o + 64), ACT.Copy)
+        if vmid is not None:
+            vmid()
+
+    zx = (R("Z"), lst(L_X, 10))
+
+    def ends():
+        tt(R("ZM"), zx, R("M16"), A.mult)
+        scan(R("ZS"), R("RS16"), R("ZM"), 0.0, A.mult, A.add)
+
+    def sizes(half):
+        u0 = 32 + 160 * half
+        ts(R("EB", 0, 160), (R("ZS"), lst(L_END, 10)), TINY, A.max)
+        tr(R("U", u0, u0 + 160), R("EB", 0, 160))
+        tr(R("EB", 160, 352), R("U", u0 - 16, u0 + 176))
+        if half == 0:
+            act(R("U2", 160, 320), R("U", u0, u0 + 160), ACT.Copy, scale=BELOW)
+            act(R("U2", 0, 160), R("U", u0, u0 + 160), ACT.Copy)
+        act(R("U", u0 + 320, u0 + 480), R("U", u0, u0 + 160), ACT.Copy, scale=BELOW)
+        cp(R("GC", 16 * half, 16 * half + 16), (R("EB"), lst(L_3R, 1)))
+
+    def diag(half):
+        u0 = 32 + 160 * half
+        tt(R("Y"), (R("GC", 16 * half, 16 * half + 16), lst(L_EX16, 10)), R("FT"), A.mult)
+        tt(R("DC"), R("U", u0, u0 + 160), R("Y"), A.is_le)
+        scan(R("DG", 160 * half, 160 * half + 160), R("RS16"), R("DC"), 0.0, A.mult, A.add)
+
+    def gcol(e):
+        c = e if e < 10 else e + 6
+        return R("GC", c, c + 1)
+
+    def vsteps(steps, lo=0, hi=None):
+        def fin(k):
+            buf, a, n, e, init = steps[k]
+            h = n // 2
+            scan(R("SO", 152 * k, 152 * k + h), R("CB", 304 * k, 304 * k + h), R("CB", 304 * k + h, 304 * k + n), init, A.add, A.add)
+        hi = len(steps) if hi is None else hi
+        for k in range(lo, hi):
+            buf, a, n, e, init = steps[k]
+            ts(R("CB", 304 * k, 304 * k + n), R(buf, a, a + n), gcol(e), A.is_lt, 0.5, A.subtract)
+            if k > lo:
+                fin(k - 1)
+        if hi > lo:
+            fin(hi - 1)
+
+    def ssteps(steps):
+        def fin(k):
+            buf, a, n, e, sb, sa, sn, acc = steps[k]
+            act(R(sb, sa, sa + sn), R(sb, sa, sa + sn), ACT.Relu, accum=acc)
+        for k, (buf, a, n, e, sb, sa, sn, acc) in enumerate(steps):
+            act(R(sb, sa, sa + n), R(buf, a, a + n), ACT.Sign, bias=gcol(e), scale=-1.0)
+            if k >= 1:
+                fin(k - 1)
+        if steps:
+            fin(len(steps) - 1)
+
+    def stayers_s(lo, hi):
+        ssteps([("U2", 16 * m + 16, 144, m, "SB2", 144 * m, 144, R("SB", W * m + 305, W * m + 306)) for m in range(lo, hi)])
+
+    def dgc(e):
+        return R("DG", 16 * e + 15, 16 * e + 16)
+
+    def planes(a, n):
+        for t in range(4):
+            act(R("XP", 320 * t + a, 320 * t + a + n), R("X", 16 + 4 * a + t, 16 + 4 * (a + n), 4), ACT.Copy)
+
+    def scatter(lo, hi):
+        win, off, src = R("OR", 16, 336), R("OFFS", lo, hi), R("IO", 16 * lo, 16 * hi)
+        emit("v", lambda e: e.tensor_copy(ap(win).indirect(ap(off)), ap(src)), [off, src], [win])
+
+    def order(rnd):
+        ns = NS0 if rnd == 0 else NS
+        ssteps([("U", 192, 160, e, "SB", W * e + 144, 162, R("ACC", e, e + 1)) for e in range(10)])
+        diag(1)
+        if ns > 10:
+            cp(R("SB", W * 10 + 304, W * ns, W), R("DG", 175, 16 * ns, 16))
+            ssteps([("U", 48 + 16 * e, 304, e, "SB", W * e, 305, R("ACC", e, e + 1)) for e in range(10, ns)])
+        vsteps([("U", 48 + 16 * e, 304, e, dgc(e)) for e in range(ns, 20)])
+        cp(R("OFFS", 0, 10), R("ACC", 0, 10))
+        ts(R("OFFS", ns, 20), R("SO", 151, 152 * (20 - ns), 152), 152.0, A.add)
+        scatter(0, 10)
+        if ns > 10:
+            cp(R("OFFS", 10, ns), R("ACC", 10, ns))
+        if rnd == 0:
+            planes(0, 320)
+        else:
+            planes(160, 160)
+        scatter(10, 20)
+        tr(R("TT", 0, 320), R("OR", 16, 336))
+        tr(R("TT", 320, 672), R("OR"))
+        ts(R("OG"), (R("TT"), lst(L_3G, 2)), 160.0, A.add)
+        for t, q in ((0, "s"), (2, "v"), (1, "s"), (3, "v")):
+            gat(q, R("G", t, 1280, 4), R("XP", 320 * t, 320 * t + 320), R("OG", 0, 20))
+
+    def thresholds():
+        tr(R("TD"), R("DS", 0, 320, 2))
+        ts(R("TH", 0, 40, 4), R("TD", 0, 160, 16), 0.75, A.mult)
+        ts(R("TH", 1, 40, 4), R("TD", 0, 160, 16), 0.25, A.mult)
+        ts(R("TH", 2, 40, 4), R("TD", 0, 160, 16), 0.75, A.mult, -BELOW, A.mult)
+        ts(R("TH", 3, 40, 4), R("TD", 0, 160, 16), 0.25, A.mult, -BELOW, A.mult)
+
+    def offsets(out, pos):
+        for t in range(4):
+            ts(R(out, 16 * t, 16 * t + 10), R(pos, 15, 160, 16), 4.0, A.mult, 640.0 + t, A.add)
+
+    def finish(half):
+        a = 160 * half
+        quant("QF", "SF", a, 160, R("X", 16 + 4 * a, 16 + 4 * a + 640))
+        bk = nextbank()
+        mm(bk, 160, "QW", "SW", 0, "QF", "SF", a)
+        dma("y", T.oc[:, 4 * a:4 * a + 640], T.QF[:, a:a + 160].bitcast(dt.uint8), [R("QF", a, a + 160)], [])
+        for k in range(4):
+            dma("s" if (half == 1 and k >= 2) else "y", T.osc[4 * k:4 * k + 4, a:a + 160], T.SF[32 * k:32 * k + 4, a:a + 160], [R("SF", a, a + 160)], [])
+        cp(R("YO", a, a + 160), R("PS", 512 * bk, 512 * bk + 160))
+        dma("s" if half == 1 else "y", T.y[:, a:a + 160], T.YO[:, a:a + 160], [R("YO", a, a + 160)], [])
+
+    gram("X", R("X", 0, 656), 0, 164, L_PS, 16, 4, PLAN_X, vmid=setup2)
+    setup4()
+    ends()
+    sizes(0)
+    nsent = 0
+    late = [None]
+    for rnd in range(3):
+        if rnd == 0:
+            def vmid0():
+                diag(0)
+                setup3()
+                cp(R("SB", 304, W * 10, W), R("DG", 15, 160, 16))
+            gram("X", R("X", 656, 1296), 164, 160, L_PK, 656, 4, PLAN_X, smid2=lambda: stayers_s(0, 2), vmid=vmid0)
+            stayers_s(2, 6)
+            ends()
+            sizes(1)
+            stayers_s(6, 10)
+        else:
+            gram("X", R("X", 656, 1296), 164, 160, L_PK, 656, 4, PLAN_K, vmid=late[0])
+            ends()
+            sizes(1)
+        order(rnd)
+        gram("G", R("G"), 4, 320, L_PA, 4, 8, PLAN_N, smid=lambda: gat("s", R("DS"), R("U", 32, 352), R("OG", 0, 20)), vmid=thresholds)
+        if rnd == 2:
+            act(R("OLF"), R("OR", 16, 336), ACT.Identity, bias=160.0)
+            dma("y", T.ol[:], T.OLF[0:128:16, :], [R("OLF")], [])
+        ends()
+        tt(R("CMP"), (R("ZS"), lst(L_N, 3)), R("TH"), A.is_ge)
+        scan(R("CS"), R("RS4"), R("CMP"), 0.0, A.mult, A.add)
+        ts(R("EC"), (R("CS"), lst(L_LC, 10)), -0.5, A.mult, 1.0, A.add)
+        tr(R("D0", 1, 320, 2), R("EC"))
+        for t in range(4):
+            scan(R("AR", t, 1280, 4), R("D0"), R("G", t, 1280, 4), 0.0, A.mult, A.add)
+        gram("AR", R("AR"), 4, 320, L_PR, 4, 8, PLAN_E, vmid=lambda: tt(R("DA"), R("TD"), R("NEG"), A.add))
+        tt(R("SD"), zx, R("DA"), A.is_lt)
+        tr(R("ST"), R("SD"))
+        scan(R("PM"), R("LM"), R("ST"), -1000.0, A.max, A.subtract)
+        offsets("OM", "PM")
+        for t, q in ((0, "s"), (2, "v"), (1, "s"), (3, "v")):
+            gat(q, R("M", t, 640, 4), R("AR"), R("OM", 16 * t, 16 * t + 10))
+        tq = quant("QM%d" % rnd, "SM%d" % rnd, 0, 160, R("M"))
+        dst = T.cores[(rank + STEP[rnd]) % len(T.cores)]
+        rid, pid, _ = topo.addr(dst)
+        mask = topo.mask(core, dst)
+        ne = len(topo.engines(core, dst))
+        wait("g", tq)
+        g.remote_dma(T["LC%d" % rnd][:].bitcast(dt.uint8), T["QM%d" % rnd][:].bitcast(dt.uint8), T.sem["arr%d" % rnd], T.sem.sent, pid, rid, mask)
+        g.remote_dma(T["LS%d" % rnd][:], T["SM%d" % rnd][:], T.sem["arr%d" % rnd], T.sem.sent, pid, rid, mask)
+        nsent += 2 * ne
+        scan(R("PT"), R("LS"), R("ST"), -1000.0, A.max, A.add)
+        if rnd < 2:
+            tt(R("ZM"), zx, R("DA"), A.min)
+            offsets("OS", "PT")
+            scan(R("ZS"), R("RS16"), R("ZM"), 0.0, A.mult, A.max)
+            for t in (0, 1):
+                gat("s", R("XP", 320 * t, 320 * t + 160), R("AR"), R("OS", 16 * t, 16 * t + 10))
+            sizes(0)
+            stayers_s(0, NSS)
+            steps = [("U2", 16 * m + 16, 144, m, 0.0) for m in range(NSS, 10)]
+            diag(0)
+            vsteps(steps, 0, len(steps) - NLATE)
+
+            def rest(steps=steps):
+                vsteps(steps, len(steps) - NLATE, len(steps))
+                cp(R("SB", 304, W * 10, W), R("DG", 15, 160, 16))
+                ts(R("SB", W * NSS + 305, W * 10, W), R("SO", 71, 152 * (10 - NSS), 152), 72.0, A.add)
+            late[0] = rest
+            for t in (2, 3):
+                gat("s", R("XP", 320 * t, 320 * t + 160), R("AR"), R("OS", 16 * t, 16 * t + 10))
+        else:
+            offsets("OS", "PT")
+            for t, q in ((0, "s"), (2, "v"), (1, "s"), (3, "v")):
+                gat(q, R("X", 16 + t, 656, 4), R("AR"), R("OS", 16 * t, 16 * t + 10))
+            quant("QW", "SW", 0, 128, R("VT"))
+            finish(0)
+        src = T.cores[(rank - STEP[rnd]) % len(T.cores)]
+        g.tensor.wait_ge(T.sem["arr%d" % rnd], 2 * len(topo.engines(src, core)))
+        banks = []
+        for b in range(4):
+            bk = nextbank()
+            banks.append(bk)
+            mm(bk, 160, "WC", "WS", 128 * b, "LC%d" % rnd, "LS%d" % rnd, 0)
+        for b in (0, 1, 2, 3):
+            o, i = R("X", 656 + b, 1296, 4), R("PS", 512 * banks[b], 512 * banks[b] + 160)
+            if b in (KV if rnd < 2 else (0, 2)):
+                ts(o, i, 0.03125, A.mult)
+            else:
+                act(o, i, ACT.Copy, scale=0.03125)
+    finish(1)
+
+    g.wait_ge(T.sem.sent, nsent)
+    for q in ("v", "s", "p", "g"):
+        g.wait_ge(T.sem[sem[q]], count[q])
+    for i in range(ndma[0]):
+        g.wait_ge(T.sem["d%d" % i], 16)

@@ -4,14 +4,15 @@ F, B, U16, I32, C4, U8 = "float32", "bfloat16", "uint16", "int32", "float8_e4m3f
 STEP = [1, 2, 1]
 W = 306
 NS = 12
-NS0 = 10
+NS0 = 11
 NSS = 3
 NLATE = 1
+LAGS = 2
 KV = (0,)
 PLAN_X = "q so0 so1 so2 so3 ve0 ve1 ve2 ve3"
-PLAN_K = "ve0 vo0 ve1 vo1 ve2 so2 so3 q ve3"
+PLAN_K = "ve0 vo0 ve1 vo1 ve2 so2 so3 ve3 q"
 PLAN_N = "ve2 so0 so1 so2 q ve0 ve1 ve3 vo3"
-PLAN_E = "so0 se0 so1 se1 so2 so3 q ve2 ve3"
+PLAN_E = "so0 so1 so2 so3 ve0 ve1 ve2 ve3 q"
 TINY = 2.0 ** -100
 BELOW = 1.0 - 2.0 ** -24
 FAR = -1.0e25
@@ -25,7 +26,8 @@ SCRATCH = {
     "X": _sb(1296, B), "XP": _sb(1280, B), "G": _sb(1280, B), "AR": _sb(1280, B), "MV": _sb(1280, B), "M": _sb(640, B), "VT": _sb(512, B),
     "QU": _sb(324, C4), "SU": _sb(324, U8), "QS": _sb(640, C4), "SS": _sb(640, U8), "QV": _sb(320, C4), "SV": _sb(320, U8),
     "WC": _sb(512, C4), "WS": _sb(512, U8), "QW": _sb(128, C4), "SW": _sb(128, U8), "QF": _sb(320, C4), "SF": _sb(320, U8),
-    "Z": _sb(320, F), "ZM": _sb(160, F), "ZS": _sb(160, F), "EB": _sb(352, F), "U": _sb(672, F), "U2": _sb(320, F), "GC": _sb(32, F),
+    "Z": _sb(320, F), "ZM": _sb(160, F), "ZS": _sb(160, F), "EB": _sb(160, F), "U": _sb(672, F), "U2": _sb(320, F),
+    "GT": _sb(160, F), "GS": _sb(320, F), "RT": _sb(160, F), "BIGF": _sb(160, F),
     "Y": _sb(160, F), "DC": _sb(160, B), "DG": _sb(320, B), "CB": _sb(12 * 304, B), "SO": _sb(12 * 152, B),
     "SB": _sb(14 * W, F), "SB2": _sb(10 * 144, F), "ACC": _sb(16, F), "OFFS": _sb(20, U16), "OR": _sb(352, B), "TT": _sb(672, B),
     "OG": _sb(32, U16), "DS": _sb(320, F), "TD": _sb(160, F), "DA": _sb(160, F), "TH": _sb(48, F),
@@ -47,9 +49,9 @@ NDMA = 24
 SEMAPHORES = ["cv", "cs", "cp", "cg", "sent", "arr0", "arr1", "arr2"] + ["d%d" % _i for _i in range(NDMA)]
 
 L_PS, L_PK, L_PA, L_PR = 0, 40, 80, 120
-L_END, L_EX16, L_LC, L_X = 160, 170, 180, 190
-L_N, L_3R, L_3G = 200, 204, 206
-C16, CH, CU, C32, C4Q, CE, CNE, CX16, C64, C2X, CT4, CT5 = 1, 2, 3, 4, 5, 6, 7, 8, 9, 10, 11, 12
+L_END, L_LC, L_X = 160, 170, 190
+L_N, L_3G = 200, 206
+C16, CH, CU, C32, C4Q, CE, CNE, CX16, C64, C2X, CT4 = 1, 2, 3, 4, 5, 6, 7, 8, 9, 10, 11
 
 
 def rank_program(g, core, T, topo):
@@ -227,15 +229,15 @@ def rank_program(g, core, T, topo):
     iota(R("J40"), [[32, 5], [0, 4], [16, 2]], 0)
     mset(R("X", 0, 16), 0.0)
     mset(R("ONEB"), 1.0)
-    mset(R("U", 16, 208), 0.0)
+    mset(R("BIGF"), 1.0e29)
     for a in range(4):
         asel(R("JM"), R("J40"), [[0, 5], [1, 4], [0, 2]], A.is_equal, -1000.0, -a, 0, quarter=a)
     iota(R("KI", 30, 40), [[64, 5], [1, 2]], 0)
     iota(R("FT0"), p16, 0)
     iota(R("KI", 0, 10), [[16, 10]], 15)
-    iota(R("KI", 10, 20), [[1, 10]], 0)
-    iota(R("KI", 20, 30), [[4, 10]], 3)
+    iota(R("KI", 10, 20), [[4, 10]], 3)
     asel(R("RS16"), R("ONEB"), p16, A.not_equal, 0.0, 0, 0)
+    asel(R("RT"), R("BIGF"), p16, A.not_equal, TINY, 0, 0)
     iota(R("KK", 0, 2), [[256, 2]], 0)
     iota(R("KK", 4, 8), [[4, 4]], 0)
     iota(R("LA"), [[32, 10], [0, 16]], -159)
@@ -255,28 +257,29 @@ def rank_program(g, core, T, topo):
     ts(col(C2X), col(C16), 2.0, A.mult)
     cp(R("MK", 1, 2), col(CH))
     ts(col(CE), col(CH), -1.0, A.mult, 1.0, A.add)
-    ts(col(CT5), col(CNE), 176.0, A.mult, col(CX16), A.add)
     ts(col(CT4), col(CNE), 336.0, A.mult, col(CX16), A.add)
     mset(R("TH"), 0.0)
     ts(R("JF"), R("JM"), col(C16), A.add)
-    ts(lst(L_3R, 1), col(CT5), 351.0, A.min)
+    ts(lst(L_X, 10), R("KI", 30, 40), col(C64), A.add)
     ts(lst(L_PS, 40), R("JF"), 4.0, A.add, 0.0, A.max)
     ts(lst(L_PK, 40), R("JF"), 164.0, A.add, 0.0, A.max)
     act(R("J2"), R("JF"), ACT.Copy, scale=2.0)
-    ts(lst(L_X, 10), R("KI", 30, 40), col(C64), A.add)
     ts(lst(L_PA, 40), R("J2"), 4.0, A.add, 0.0, A.max)
     ts(lst(L_PR, 40), R("J2"), 5.0, A.add, 0.0, A.max)
 
     def setup2():
         ts(R("M16"), R("FT0"), col(C16), A.is_equal)
-        cp(lst(L_END, 30), R("KI", 0, 30))
+        cp(lst(L_END, 20), R("KI", 0, 20))
         ts(R("FT1"), R("FT0"), col(C16), A.is_ge, -2.0 ** -24, A.mult)
         act(R("FT"), R("FT1"), ACT.Identity, bias=1.0)
 
     def setup3():
         ts(R("LT"), R("KK", 4, 8), col(C4Q), A.add, 16.0, A.mult)
         ts(lst(L_3G, 2), R("KK", 0, 2), col(CT4), A.add, 671.0, A.min)
-        ts(lst(L_N, 4), R("LT"), 15.0, A.add, 159.0, A.min)
+
+    def setup3b():
+        ts(lst(L_N, 1), R("LT", 0, 1), 15.0, A.add, 159.0, A.min)
+        ts(lst(L_N + 2, 2), R("LT", 1, 3), 15.0, A.add, 159.0, A.min)
 
     def setup4():
         act(R("NEG0"), R("M16"), ACT.Identity, bias=FAR, scale=-FAR)
@@ -301,7 +304,7 @@ def rank_program(g, core, T, topo):
                 ts(o, i, R("MK", h, h + 1), A.mult)
         quant("QV", "SV", 0, 320, R("MV"))
         banks = []
-        for lo, hi in ((0, 3), (3, 5)):
+        for lo, hi in ((0, 2), (2, 5)):
             off = lst(plist + 8 * lo, 8 * (hi - lo))
             oc, os_ = R("QS", 128 * lo, 128 * hi), R("SS", 128 * lo, 128 * hi)
             emit("s", lambda e: e.activation(ap(os_), T.SU[:, 0:324].indirect(ap(off)), ACT.Copy), [R("SU"), off], [os_])
@@ -320,46 +323,75 @@ def rank_program(g, core, T, topo):
         if vmid is not None:
             vmid()
 
-    zx = (R("Z"), lst(L_X, 10))
+    zpart = [((R("Z", 0, 128), lst(L_X, 4)), 0, 64), ((R("Z"), lst(L_X + 4, 6)), 64, 160), ((R("Z"), lst(L_X, 10)), 0, 160)]
 
-    def ends():
-        tt(R("ZM"), zx, R("M16"), A.mult)
-        scan(R("ZS"), R("RS16"), R("ZM"), 0.0, A.mult, A.add)
+    def zm(k, other="M16", op=A.mult, out="ZM"):
+        z, a, b = zpart[k]
+        tt(R(out, a, b), z, R(other, a, b), op)
+
+    def zs(k, op=A.add):
+        z, a, b = zpart[k]
+        scan(R("ZS", a, b), R("RS16", a, b), R("ZM", a, b), 0.0, A.mult, op)
+
+    def gt(k, src="ZM", out="GT"):
+        z, a, b = zpart[k]
+        tr(R(out, a, b), R(src, a, b))
+
+    def eb(k):
+        z, a, b = zpart[k]
+        ts(R("EB", a, b), (R("ZS", 0, b), lst(L_END + a // 16, (b - a) // 16)), TINY, A.max)
+
+    def gs(k, half):
+        z, a, b = zpart[k]
+        scan(R("GS", 160 * half + a, 160 * half + b), R("RT", a, b), R("GT", a, b), 1.0, A.min, A.max)
+
+    def row(k, half):
+        z, a, b = zpart[k]
+        tr(R("U2", a, b) if half == 0 else R("U", 192 + a, 192 + b), R("EB", a, b))
+
+    def below(half):
+        if half == 1:
+            ts(R("U", 512, 672), R("U", 192, 352), BELOW, A.mult)
+            return
+        ts(R("U2", 160, 320), R("U2", 0, 160), BELOW, A.mult)
+        act(R("U", 352, 512), R("U2", 0, 160), ACT.Copy, scale=BELOW)
+        act(R("U", 32, 192), R("U2", 0, 160), ACT.Copy)
 
     def sizes(half):
-        u0 = 32 + 160 * half
-        ts(R("EB", 0, 160), (R("ZS"), lst(L_END, 10)), TINY, A.max)
-        tr(R("U", u0, u0 + 160), R("EB", 0, 160))
-        tr(R("EB", 160, 352), R("U", u0 - 16, u0 + 176))
-        if half == 0:
-            act(R("U2", 160, 320), R("U", u0, u0 + 160), ACT.Copy, scale=BELOW)
-            act(R("U2", 0, 160), R("U", u0, u0 + 160), ACT.Copy)
-        act(R("U", u0 + 320, u0 + 480), R("U", u0, u0 + 160), ACT.Copy, scale=BELOW)
-        cp(R("GC", 16 * half, 16 * half + 16), (R("EB"), lst(L_3R, 1)))
+        zs(2, A.max)
+        gt(2)
+        eb(2)
+        gs(2, half)
+        row(2, half)
 
     def diag(half):
-        u0 = 32 + 160 * half
-        tt(R("Y"), (R("GC", 16 * half, 16 * half + 16), lst(L_EX16, 10)), R("FT"), A.mult)
-        tt(R("DC"), R("U", u0, u0 + 160), R("Y"), A.is_le)
-        scan(R("DG", 160 * half, 160 * half + 160), R("RS16"), R("DC"), 0.0, A.mult, A.add)
+        return [lambda: tt(R("Y"), (R("GS", 160 * half, 160 * half + 160), lst(L_END, 10)), R("FT"), A.mult),
+                lambda: tt(R("DC"), R("U", 192, 352) if half else R("U2", 0, 160), R("Y"), A.is_le),
+                lambda: scan(R("DG", 160 * half, 160 * half + 160), R("RS16"), R("DC"), 0.0, A.mult, A.add)]
 
     def gcol(e):
-        c = e if e < 10 else e + 6
-        return R("GC", c, c + 1)
+        return R("GS", 16 * e + 15, 16 * e + 16)
 
-    def vsteps(steps, lo=0, hi=None):
+    def vsteps(steps, lo=0, hi=None, between=()):
         def fin(k):
             buf, a, n, e, init = steps[k]
             h = n // 2
             scan(R("SO", 152 * k, 152 * k + h), R("CB", 304 * k, 304 * k + h), R("CB", 304 * k + h, 304 * k + n), init, A.add, A.add)
         hi = len(steps) if hi is None else hi
+        between = list(between)
+        nxt = lo
         for k in range(lo, hi):
             buf, a, n, e, init = steps[k]
             ts(R("CB", 304 * k, 304 * k + n), R(buf, a, a + n), gcol(e), A.is_lt, 0.5, A.subtract)
-            if k > lo:
-                fin(k - 1)
-        if hi > lo:
-            fin(hi - 1)
+            if between:
+                between.pop(0)()
+            else:
+                for _ in range(2):
+                    if nxt < k:
+                        fin(nxt)
+                        nxt += 1
+        for k in range(nxt, hi):
+            fin(k)
 
     def ssteps(steps):
         def fin(k):
@@ -367,10 +399,10 @@ def rank_program(g, core, T, topo):
             act(R(sb, sa, sa + sn), R(sb, sa, sa + sn), ACT.Relu, accum=acc)
         for k, (buf, a, n, e, sb, sa, sn, acc) in enumerate(steps):
             act(R(sb, sa, sa + n), R(buf, a, a + n), ACT.Sign, bias=gcol(e), scale=-1.0)
-            if k >= 1:
-                fin(k - 1)
-        if steps:
-            fin(len(steps) - 1)
+            if k >= LAGS:
+                fin(k - LAGS)
+        for k in range(max(0, len(steps) - LAGS), len(steps)):
+            fin(k)
 
     def stayers_s(lo, hi):
         ssteps([("U2", 16 * m + 16, 144, m, "SB2", 144 * m, 144, R("SB", W * m + 305, W * m + 306)) for m in range(lo, hi)])
@@ -389,11 +421,17 @@ def rank_program(g, core, T, topo):
     def order(rnd):
         ns = NS0 if rnd == 0 else NS
         ssteps([("U", 192, 160, e, "SB", W * e + 144, 162, R("ACC", e, e + 1)) for e in range(10)])
-        diag(1)
+        d = diag(1)
+        d[0]()
+        below(1)
+        d[1]()
+        bt = [d[2]]
         if ns > 10:
-            cp(R("SB", W * 10 + 304, W * ns, W), R("DG", 175, 16 * ns, 16))
-            ssteps([("U", 48 + 16 * e, 304, e, "SB", W * e, 305, R("ACC", e, e + 1)) for e in range(10, ns)])
-        vsteps([("U", 48 + 16 * e, 304, e, dgc(e)) for e in range(ns, 20)])
+            def longs():
+                cp(R("SB", W * 10 + 304, W * ns, W), R("DG", 175, 16 * ns, 16))
+                ssteps([("U", 48 + 16 * e, 304, e, "SB", W * e, 305, R("ACC", e, e + 1)) for e in range(10, ns)])
+            bt.append(longs)
+        vsteps([("U", 48 + 16 * e, 304, e, dgc(e)) for e in range(ns, 20)], between=bt)
         cp(R("OFFS", 0, 10), R("ACC", 0, 10))
         ts(R("OFFS", ns, 20), R("SO", 151, 152 * (20 - ns), 152), 152.0, A.add)
         scatter(0, 10)
@@ -416,9 +454,20 @@ def rank_program(g, core, T, topo):
         ts(R("TH", 1, 40, 4), R("TD", 0, 160, 16), 0.25, A.mult)
         ts(R("TH", 2, 40, 4), R("TD", 0, 160, 16), 0.75, A.mult, -BELOW, A.mult)
         ts(R("TH", 3, 40, 4), R("TD", 0, 160, 16), 0.25, A.mult, -BELOW, A.mult)
+        zm(0)
+        tt(R("DA"), R("TD"), R("NEG"), A.add)
+        zs(0)
 
-    def offsets(out, pos):
-        for t in range(4):
+    def rem(k, t):
+        z, a, b = zpart[k]
+        scan(R("AR", 8 * a + t, 8 * b, 4), R("D0", 2 * a, 2 * b), R("G", 8 * a + t, 8 * b, 4), 0.0, A.mult, A.add)
+
+    def emid():
+        zm(0, "DA", A.is_lt, "SD")
+        gt(0, "SD", "ST")
+
+    def offsets(out, pos, which):
+        for t in which:
             ts(R(out, 16 * t, 16 * t + 10), R(pos, 15, 160, 16), 4.0, A.mult, 640.0 + t, A.add)
 
     def finish(half):
@@ -434,44 +483,68 @@ def rank_program(g, core, T, topo):
 
     gram("X", R("X", 0, 656), 0, 164, L_PS, 16, 4, PLAN_X, vmid=setup2)
     setup4()
-    ends()
+    zm(2)
     sizes(0)
+    setup3()
+    below(0)
     nsent = 0
     late = [None]
     for rnd in range(3):
         if rnd == 0:
             def vmid0():
-                diag(0)
-                setup3()
+                d = diag(0)
+                d[0]()
+                setup3b()
+                d[1]()
+                zm(0)
+                d[2]()
+                zs(0)
+                gt(0)
                 cp(R("SB", 304, W * 10, W), R("DG", 15, 160, 16))
             gram("X", R("X", 656, 1296), 164, 160, L_PK, 656, 4, PLAN_X, smid2=lambda: stayers_s(0, 2), vmid=vmid0)
-            stayers_s(2, 6)
-            ends()
-            sizes(1)
-            stayers_s(6, 10)
+            stayers_s(2, 10)
         else:
             gram("X", R("X", 656, 1296), 164, 160, L_PK, 656, 4, PLAN_K, vmid=late[0])
-            ends()
-            sizes(1)
+        zm(1)
+        eb(0)
+        gs(0, 1)
+        zs(1)
+        gt(1)
+        row(0, 1)
+        eb(1)
+        gs(1, 1)
+        row(1, 1)
         order(rnd)
         gram("G", R("G"), 4, 320, L_PA, 4, 8, PLAN_N, smid=lambda: gat("s", R("DS"), R("U", 32, 352), R("OG", 0, 20)), vmid=thresholds)
         if rnd == 2:
             act(R("OLF"), R("OR", 16, 336), ACT.Identity, bias=160.0)
             dma("y", T.ol[:], T.OLF[0:128:16, :], [R("OLF")], [])
-        ends()
-        tt(R("CMP"), (R("ZS"), lst(L_N, 3)), R("TH"), A.is_ge)
-        scan(R("CS"), R("RS4"), R("CMP"), 0.0, A.mult, A.add)
-        ts(R("EC"), (R("CS"), lst(L_LC, 10)), -0.5, A.mult, 1.0, A.add)
-        tr(R("D0", 1, 320, 2), R("EC"))
+        zm(1)
+        tt(R("CMP", 0, 16), (R("ZS", 0, 64), lst(L_N, 1)), R("TH", 0, 16), A.is_ge)
+        zs(1)
+        scan(R("CS", 0, 16), R("RS4", 0, 16), R("CMP", 0, 16), 0.0, A.mult, A.add)
+        tt(R("CMP", 16, 48), (R("ZS"), lst(L_N + 2, 2)), R("TH", 16, 48), A.is_ge)
+        ts(R("EC", 0, 64), (R("CS", 0, 16), lst(L_LC, 4)), -0.5, A.mult, 1.0, A.add)
+        scan(R("CS", 16, 48), R("RS4", 16, 48), R("CMP", 16, 48), 0.0, A.mult, A.add)
+        tr(R("D0", 1, 128, 2), R("EC", 0, 64))
+        ts(R("EC", 64, 160), (R("CS"), lst(L_LC + 4, 6)), -0.5, A.mult, 1.0, A.add)
+        rem(0, 0)
+        rem(0, 1)
+        tr(R("D0", 129, 320, 2), R("EC", 64, 160))
+        rem(0, 2)
+        rem(0, 3)
         for t in range(4):
-            scan(R("AR", t, 1280, 4), R("D0"), R("G", t, 1280, 4), 0.0, A.mult, A.add)
-        gram("AR", R("AR"), 4, 320, L_PR, 4, 8, PLAN_E, vmid=lambda: tt(R("DA"), R("TD"), R("NEG"), A.add))
-        tt(R("SD"), zx, R("DA"), A.is_lt)
-        tr(R("ST"), R("SD"))
+            rem(1, t)
+        gram("AR", R("AR"), 4, 320, L_PR, 4, 8, PLAN_E, vmid=emid)
+        zm(1, "DA", A.is_lt, "SD")
+        gt(1, "SD", "ST")
         scan(R("PM"), R("LM"), R("ST"), -1000.0, A.max, A.subtract)
-        offsets("OM", "PM")
+        scan(R("PT"), R("LS"), R("ST"), -1000.0, A.max, A.add)
+        offsets("OM", "PM", (0, 2, 1, 3))
+        offsets("OS", "PT", (0,))
         for t, q in ((0, "s"), (2, "v"), (1, "s"), (3, "v")):
             gat(q, R("M", t, 640, 4), R("AR"), R("OM", 16 * t, 16 * t + 10))
+        offsets("OS", "PT", (1, 2))
         tq = quant("QM%d" % rnd, "SM%d" % rnd, 0, 160, R("M"))
         dst = T.cores[(rank + STEP[rnd]) % len(T.cores)]
         rid, pid, _ = topo.addr(dst)
@@ -481,28 +554,30 @@ def rank_program(g, core, T, topo):
         g.remote_dma(T["LC%d" % rnd][:].bitcast(dt.uint8), T["QM%d" % rnd][:].bitcast(dt.uint8), T.sem["arr%d" % rnd], T.sem.sent, pid, rid, mask)
         g.remote_dma(T["LS%d" % rnd][:], T["SM%d" % rnd][:], T.sem["arr%d" % rnd], T.sem.sent, pid, rid, mask)
         nsent += 2 * ne
-        scan(R("PT"), R("LS"), R("ST"), -1000.0, A.max, A.add)
         if rnd < 2:
-            tt(R("ZM"), zx, R("DA"), A.min)
-            offsets("OS", "PT")
-            scan(R("ZS"), R("RS16"), R("ZM"), 0.0, A.mult, A.max)
-            for t in (0, 1):
+            zm(2, "DA", A.min)
+            offsets("OS", "PT", (3,))
+            for t in (0, 1, 2):
                 gat("s", R("XP", 320 * t, 320 * t + 160), R("AR"), R("OS", 16 * t, 16 * t + 10))
             sizes(0)
+            d = diag(0)
+            d[0]()
+            below(0)
+            d[1]()
             stayers_s(0, NSS)
             steps = [("U2", 16 * m + 16, 144, m, 0.0) for m in range(NSS, 10)]
-            diag(0)
-            vsteps(steps, 0, len(steps) - NLATE)
+            vsteps(steps, 0, len(steps) - NLATE, between=[lambda: None, d[2]])
 
             def rest(steps=steps):
-                vsteps(steps, len(steps) - NLATE, len(steps))
+                vsteps(steps, len(steps) - NLATE, len(steps), between=[lambda: zm(0)])
                 cp(R("SB", 304, W * 10, W), R("DG", 15, 160, 16))
+                zs(0)
+                gt(0)
                 ts(R("SB", W * NSS + 305, W * 10, W), R("SO", 71, 152 * (10 - NSS), 152), 72.0, A.add)
             late[0] = rest
-            for t in (2, 3):
-                gat("s", R("XP", 320 * t, 320 * t + 160), R("AR"), R("OS", 16 * t, 16 * t + 10))
+            gat("s", R("XP", 960, 1120), R("AR"), R("OS", 48, 58))
         else:
-            offsets("OS", "PT")
+            offsets("OS", "PT", (3,))
             for t, q in ((0, "s"), (2, "v"), (1, "s"), (3, "v")):
                 gat(q, R("X", 16 + t, 656, 4), R("AR"), R("OS", 16 * t, 16 * t + 10))
             quant("QW", "SW", 0, 128, R("VT"))

@@ -1,57 +1,127 @@
+import numpy as np
 from concourse.mybir import dt, AluOpType, ActivationFunctionType
 
 F, B, U16, I32, C4, U8 = "float32", "bfloat16", "uint16", "int32", "float8_e4m3fn_x4", "uint8"
 STEP = [1, 2, 1]
+CUT = 96
 W = 306
-NS = 12
-NS0 = 11
-NSS = 3
-NLATE = 1
-LAGS = 2
-KV = (0,)
-PLAN_X = "q so0 so1 so2 so3 ve0 ve1 ve2 ve3"
-PLAN_K = "ve0 vo0 ve1 vo1 ve2 so2 so3 ve3 q"
-PLAN_N = "ve2 so0 so1 so2 q ve0 ve1 ve3 vo3"
-PLAN_E = "so0 so1 so2 so3 ve0 ve1 ve2 ve3 q"
+NK = [6, 6, 6]
+NS = [6, 6, 6]
 TINY = 2.0 ** -100
 BELOW = 1.0 - 2.0 ** -24
 FAR = -1.0e25
+FREE = -200.0
+CYC, GAT, SCA, LAG, DMA, HOP, ONCE = 0.00092, 1.56, 3.5, 0.18, 1.8, 2.4, 2.0
+SPARE, TURNS, SHAKES, SEED = 0.7, 2, 2500, 1
+TAIL = 1
+PLANNED = []
+LEN = []
 
 
 def _sb(n, d):
     return ("sbuf", [128, n], d)
 
 
+PIECES = ((0, CUT), (CUT, 160))
 SCRATCH = {
-    "X": _sb(1296, B), "XP": _sb(1280, B), "G": _sb(1280, B), "AR": _sb(1280, B), "MV": _sb(1280, B), "M": _sb(640, B), "VT": _sb(512, B),
-    "QU": _sb(324, C4), "SU": _sb(324, U8), "QS": _sb(640, C4), "SS": _sb(640, U8), "QV": _sb(320, C4), "SV": _sb(320, U8),
-    "WC": _sb(512, C4), "WS": _sb(512, U8), "QW": _sb(128, C4), "SW": _sb(128, U8), "QF": _sb(320, C4), "SF": _sb(320, U8),
-    "Z": _sb(320, F), "ZM": _sb(160, F), "ZS": _sb(160, F), "EB": _sb(160, F), "U": _sb(672, F), "U2": _sb(320, F),
-    "GT": _sb(160, F), "GS": _sb(320, F), "RT": _sb(160, F), "BIGF": _sb(160, F),
-    "Y": _sb(160, F), "DC": _sb(160, B), "DG": _sb(320, B), "CB": _sb(12 * 304, B), "SO": _sb(12 * 152, B),
-    "SB": _sb(14 * W, F), "SB2": _sb(10 * 144, F), "ACC": _sb(16, F), "OFFS": _sb(20, U16), "OR": _sb(352, B), "TT": _sb(672, B),
-    "OG": _sb(32, U16), "DS": _sb(320, F), "TD": _sb(160, F), "DA": _sb(160, F), "TH": _sb(48, F),
-    "CMP": _sb(48, F), "CS": _sb(48, F), "EC": _sb(160, B), "D0": _sb(320, B), "SD": _sb(160, B), "ST": _sb(160, B),
-    "PM": _sb(160, B), "PT": _sb(160, B), "OM": _sb(64, U16), "OS": _sb(64, U16),
+    "X": _sb(1296, B), "XP": _sb(1280, B), "G": _sb(1296, B), "AR": _sb(1296, B), "M": _sb(896, B), "VT": _sb(512, B),
+    "WC": _sb(512, C4), "WS": _sb(512, U8), "QW": _sb(128, C4), "SW": _sb(128, U8), "QF": _sb(416, C4), "SF": _sb(416, U8),
+    "QM": _sb(768, C4), "SM": _sb(768, U8), "LC": _sb(608, C4), "LS": _sb(608, U8),
+    "UU": _sb(480, F), "DS": _sb(640, F), "GS": _sb(320, F), "RT": _sb(160, F),
+    "ZM": _sb(480, F), "ZS": _sb(480, F), "EB": _sb(320, F), "GT": _sb(320, F), "Y": _sb(320, F), "DC": _sb(320, B), "DG": _sb(320, B),
+    "CB": _sb(20 * 304, B), "SO": _sb(20 * 152, B), "SB": _sb(20 * W, F), "ACC": _sb(20, F), "OFFS": _sb(20, U16),
+    "ORK": _sb(960, B), "FL": _sb(320, B), "CU": _sb(320, B), "VAL": _sb(352, B), "TT": _sb(896, B), "OG": _sb(32, U16),
+    "ORS": _sb(192, B), "TS": _sb(352, B), "OS": _sb(96, U16), "FS": _sb(160, B), "VS": _sb(160, B), "OLW": _sb(320, B), "JR": _sb(320, B),
+    "TD": _sb(160, F), "DA": _sb(160, F), "TH": _sb(64, F), "CMP": _sb(64, F), "CS": _sb(64, F), "EC": _sb(160, B), "D0": _sb(320, B),
+    "SD": _sb(160, B), "ST": _sb(160, B), "PM": _sb(160, B), "PT": _sb(160, B), "OM": _sb(64, U16),
     "YO": _sb(320, F), "OLF": _sb(320, F),
-    "PI": _sb(8, I32), "COL": _sb(24, F), "MK": _sb(2, B), "J40": _sb(40, F), "JM": _sb(40, F), "JF": _sb(40, F), "J2": _sb(40, F), "LST": _sb(224, U16),
-    "RS16": _sb(160, B), "ONEB": _sb(160, B), "RS4": _sb(48, B), "FT0": _sb(160, F), "FT1": _sb(160, F), "FT": _sb(160, F),
-    "M16": _sb(160, F), "NEG0": _sb(160, F), "NEG": _sb(160, F), "LA": _sb(160, F), "LB": _sb(160, B), "LB2": _sb(160, B), "LM": _sb(160, B), "LS": _sb(160, B),
-    "IO": _sb(320, B), "KI": _sb(48, F), "KK": _sb(8, F), "LT": _sb(4, F),
+    "PI": _sb(8, I32), "COL": _sb(24, F), "MK": _sb(2, B), "J40": _sb(40, F), "A40": _sb(40, F), "JM": _sb(40, F), "JF": _sb(40, F),
+    "LF": _sb(224, F), "LST": _sb(224, U16), "RS16": _sb(160, B), "RS4": _sb(64, B), "FT0": _sb(160, F), "FT1": _sb(160, F), "FT": _sb(160, F),
+    "M16": _sb(160, F), "DM": _sb(160, F), "LM": _sb(320, B), "LT": _sb(4, F),
     "PS": ("psum", [128, 4096], F),
 }
-for _r in range(3):
-    SCRATCH["QM%d" % _r] = _sb(160, C4)
-    SCRATCH["SM%d" % _r] = _sb(160, U8)
-    SCRATCH["LC%d" % _r] = _sb(160, C4)
-    SCRATCH["LS%d" % _r] = _sb(160, U8)
-NDMA = 24
-SEMAPHORES = ["cv", "cs", "cp", "cg", "sent", "arr0", "arr1", "arr2"] + ["d%d" % _i for _i in range(NDMA)]
+for _k in "dne":
+    SCRATCH["QU" + _k] = _sb(324, C4)
+    SCRATCH["SU" + _k] = _sb(324, U8)
+    SCRATCH["MV" + _k] = _sb(1280, B)
+    SCRATCH["QV" + _k] = _sb(320, C4)
+    SCRATCH["SV" + _k] = _sb(320, U8)
+    SCRATCH["QS" + _k] = _sb(640, C4)
+    SCRATCH["SS" + _k] = _sb(640, U8)
+    SCRATCH["Z" + _k] = _sb(320, F)
+NDMA = 26
+SEMAPHORES = ["cv", "cs", "cp", "cg", "sent"] + ["arr%d" % _i for _i in range(6)] + ["d%d" % _i for _i in range(NDMA)]
+BANKS = ((0, 1, 2, 3), (4, 5, 6, 7))
 
-L_PS, L_PK, L_PA, L_PR = 0, 40, 80, 120
-L_END, L_LC, L_X = 160, 170, 190
-L_N, L_3G = 200, 206
-C16, CH, CU, C32, C4Q, CE, CNE, CX16, C64, C2X, CT4 = 1, 2, 3, 4, 5, 6, 7, 8, 9, 10, 11
+L_PS, L_PK, L_XB, L_END = 0, 40, 80, 90
+L_PA, L_PR, L_LC, L_X, L_N, L_3G, L_3S = 100, 140, 180, 190, 200, 204, 208
+C16, CH, CU, C32, C4Q, CQ, CE, CNE, CX16, C64, CM, CT, CG0, CG1, CS1 = range(1, 16)
+
+
+def plan(nodes):
+    if PLANNED:
+        return [(nodes[i], q) for i, q in PLANNED]
+    num = len(nodes)
+    deps = [[p["nr"] for p in n["deps"]] for n in nodes]
+    nxt = [[p["nr"] for p in n["next"]] for n in nodes]
+    opts = [[(q, c) for q, (f, c) in n["opts"].items()] for n in nodes]
+    lat = [n["lat"] for n in nodes]
+
+    def fill(rank, lean, after, early):
+        first = {q: [] for q in "vspgy"}
+        last = {q: [] for q in "vspgy"}
+        end, start, queue = [0.0] * num, [0.0] * num, [None] * num
+        for i in sorted(range(num), key=lambda i: -rank[i]):
+            ready = max([end[p] + LAG for p in after[i]], default=0.0) + (0.0 if early else lat[i])
+            best = None
+            for q, c in opts[i]:
+                a, b = first[q], last[q]
+                k = len(b)
+                while k and b[k - 1] > ready:
+                    k -= 1
+                t = ready
+                while k < len(a) and t + c > a[k]:
+                    t = max(t, b[k])
+                    k += 1
+                worth = t + c + (lean[i] if q == "v" else 0.0)
+                if best is None or worth < best[0]:
+                    best = (worth, t, q, c, k)
+            worth, t, q, c, k = best
+            first[q].insert(k, t)
+            last[q].insert(k, t + c)
+            start[i], end[i], queue[i] = t, t + c + (lat[i] if early else 0.0), q
+        return end, start, queue
+
+    def tighten(rank, lean):
+        return fill(fill(rank, lean, deps, True)[0], lean, nxt, False)[0]
+
+    rank = [0.0] * num
+    for i in reversed(range(num)):
+        rank[i] = min(c for q, c in opts[i]) + lat[i] + max([LAG + rank[s] for s in nxt[i]], default=0.0)
+    lean = [SPARE * dict(o).get("v", 0.0) for o in opts]
+    for _ in range(TURNS):
+        rank = tighten(rank, lean)
+    now = fill(rank, lean, deps, True)
+    rng = np.random.RandomState(SEED)
+    for step in range(SHAKES):
+        t0 = rng.uniform(0.0, max(now[0]))
+        t1 = t0 + (2.0, 4.0, 8.0)[step % 3]
+        r, l = list(rank), list(lean)
+        for i in reversed(range(num)):
+            if t0 <= now[1][i] <= t1:
+                r[i] += float(rng.normal(0.0, 0.25))
+                if len(opts[i]) > 1 and rng.uniform() < 0.2:
+                    l[i] = (-0.3, 0.0, 0.1, 0.3, 1.0)[rng.randint(5)]
+            for s in nxt[i]:
+                r[i] = max(r[i], r[s] + 1e-6)
+        if step % 4 == 0:
+            r = tighten(r, l)
+        new = fill(r, l, deps, True)
+        if max(new[0]) <= max(now[0]) + 0.03 * (1.0 - step / SHAKES):
+            rank, lean, now = r, l, new
+    PLANNED.extend((i, now[2][i]) for i in sorted(range(num), key=lambda i: (now[1][i], i)))
+    LEN.append(max(now[0]))
+    return plan(nodes)
 
 
 def rank_program(g, core, T, topo):
@@ -62,11 +132,8 @@ def rank_program(g, core, T, topo):
     ACT = ActivationFunctionType
     eng = {"v": g.vector, "s": g.scalar, "p": g.tensor, "g": g, "y": g.sync}
     sem = {"v": "cv", "s": "cs", "p": "cp", "g": "cg"}
-    count = {"v": 0, "s": 0, "p": 0, "g": 0}
-    known = {k: {} for k in eng}
+    nodes = []
     hist = {}
-    ndma = [0]
-    bank = [0]
 
     def R(name, a=0, b=None, s=1):
         n = SCRATCH[name][1][1]
@@ -77,54 +144,28 @@ def rank_program(g, core, T, topo):
             return T[r[0]][:, r[1]:r[2]]
         return T[r[0]][:, r[1]:r[2]:r[3]]
 
-    def wait(q, tok):
-        if known[q].get(tok[0], 0) < tok[1]:
-            eng[q].wait_ge(T.sem[tok[0]], tok[1])
-            for k, val in tok[2].items():
-                if known[q].get(k, 0) < val:
-                    known[q][k] = val
+    def size(r):
+        return len(range(r[1], r[2], r[3]))
 
-    def emit(q, fn, reads, writes, dma=False):
-        acc = []
-        for r in reads:
-            acc.append((r, r[0] == "PS"))
-        for r in writes:
-            acc.append((r, True))
-        need = {}
+    def call(opts, reads, writes, kind="op", lat=0.0):
+        n = {"opts": opts, "deps": [], "next": [], "kind": kind, "lat": lat, "nr": len(nodes), "w": (writes or reads)[0][0]}
+        seen = set()
         sets = []
-        for r, wr in acc:
-            if r[0] == "PS":
-                s = frozenset([r[1] // 512])
-            else:
-                s = frozenset(range(r[1], r[2], r[3]))
+        for r, wr in [(r, r[0] == "PS") for r in reads] + [(r, True) for r in writes]:
+            s = frozenset([r[1] // 512]) if r[0] == "PS" else frozenset(range(r[1], r[2], r[3]))
             sets.append((r[0], s, wr))
-            for s2, wr2, tok in hist.get(r[0], []):
-                if (wr or wr2) and known[q].get(tok[0], 0) < tok[1] and not s.isdisjoint(s2):
-                    if tok[0] not in need or need[tok[0]][1] < tok[1]:
-                        need[tok[0]] = tok
-        for tok in need.values():
-            wait(q, tok)
-        if q == "g" and count["g"] > known["g"].get("cg", 0):
-            wait("g", ("cg", count["g"], {"cg": count["g"]}))
-        ins = fn(eng[q])
-        clock = dict(known[q])
-        if dma:
-            name = "d%d" % ndma[0]
-            ndma[0] += 1
-            ins.then_inc(T.sem[name], 16)
-            clock[name] = 16
-            tok = (name, 16, clock)
-        else:
-            count[q] += 1
-            ins.then_inc(T.sem[sem[q]], 1)
-            clock[sem[q]] = count[q]
-            tok = (sem[q], count[q], clock)
+            for s2, wr2, m in hist.get(r[0], []):
+                if (wr or wr2) and m["nr"] not in seen and not s.isdisjoint(s2):
+                    seen.add(m["nr"])
+                    n["deps"].append(m)
+                    m["next"].append(n)
         for name, s, wr in sets:
             h = hist.setdefault(name, [])
             if wr:
                 h[:] = [e for e in h if not e[0] <= s]
-            h.append((s, wr, tok))
-        return tok
+            h.append((s, wr, n))
+        nodes.append(n)
+        return n
 
     def opnd(x):
         if len(x) == 2:
@@ -136,42 +177,31 @@ def rank_program(g, core, T, topo):
             return ap(x), [x]
         return x, []
 
+    def cost(out, in0, per, others=()):
+        if len(in0) == 2:
+            return 0.06 + GAT * CYC * size(out)
+        if per is None:
+            per = 0.5 if all(SCRATCH[r[0]][2] in (B, U16) for r in [out, in0] + list(others)) else 1.0
+        return CYC * max(64, per * size(out))
+
     def col(c):
         return R("COL", c, c + 1)
 
     def lst(c, n):
         return R("LST", c, c + n)
 
-    def ts(out, in0, s1, op0, s2=None, op1=None):
+    def v_ts(out, in0, s1, op0, s2=None, op1=None):
         i, rd = opnd(in0)
         a1, r1 = scal(s1)
         a2, r2 = scal(s2)
+        c = cost(out, in0, None, r1 + r2)
         if op1 is None:
-            return emit("v", lambda e: e.tensor_scalar(ap(out), i, a1, None, op0), rd + r1, [out])
-        return emit("v", lambda e: e.tensor_scalar(ap(out), i, a1, a2, op0, op1), rd + r1 + r2, [out])
+            return (lambda e: e.tensor_scalar(ap(out), i, a1, None, op0), c), rd + r1
+        return (lambda e: e.tensor_scalar(ap(out), i, a1, a2, op0, op1), c), rd + r1 + r2
 
-    def tt(out, in0, in1, op):
-        i, rd = opnd(in0)
-        return emit("v", lambda e: e.tensor_tensor(ap(out), i, ap(in1), op), rd + [in1], [out])
-
-    def cp(out, in_):
-        i, rd = opnd(in_)
-        return emit("v", lambda e: e.tensor_copy(ap(out), i), rd, [out])
-
-    def scan(out, d0, d1, init, op0, op1):
-        a, r = scal(init)
-        return emit("v", lambda e: e.tensor_tensor_scan(ap(out), ap(d0), ap(d1), a, op0, op1), [d0, d1] + r, [out])
-
-    def tr(out, in_):
-        return emit("v", lambda e: e.transpose(ap(out), ap(in_)), [in_], [out])
-
-    def mset(out, val):
-        return emit("v", lambda e: e.memset(ap(out), val), [], [out])
-
-    def act(out, in_, func, bias=None, scale=None, accum=None):
+    def s_act(out, in_, func, bias=None, scale=None, accum=None):
         i, rd = opnd(in_)
         kw = {}
-        wr = [out]
         if bias is not None:
             kw["bias"], r = scal(bias)
             rd = rd + r
@@ -180,43 +210,79 @@ def rank_program(g, core, T, topo):
             rd = rd + r
         if accum is not None:
             kw["accum_out"] = ap(accum)
-            wr = wr + [accum]
-        return emit("s", lambda e: e.activation(ap(out), i, func, **kw), rd, wr)
+        return (lambda e: e.activation(ap(out), i, func, **kw), cost(out, in_, 1.0) + (0.02 if accum else 0.0)), rd
 
-    def gat(q, out, win, off):
-        if q == "v":
-            return cp(out, (win, off))
-        return act(out, (win, off), ACT.Copy)
+    def ts(out, in0, s1, op0, s2=None, op1=None):
+        o, rd = v_ts(out, in0, s1, op0, s2, op1)
+        return call({"v": o}, rd, [out])
+
+    def act(out, in_, func, bias=None, scale=None, accum=None):
+        o, rd = s_act(out, in_, func, bias, scale, accum)
+        return call({"s": o}, rd, [out] + ([accum] if accum else []))
+
+    def either(out, v, s):
+        return call({"v": v[0], "s": s[0]}, v[1] + s[1], [out])
+
+    def v_cp(out, in_):
+        i, rd = opnd(in_)
+        return (lambda e: e.tensor_copy(ap(out), i), cost(out, in_, None)), rd
+
+    def cp(out, in_):
+        o, rd = v_cp(out, in_)
+        return call({"v": o}, rd, [out])
+
+    def move(out, in_):
+        return either(out, v_cp(out, in_), s_act(out, in_, ACT.Copy))
+
+    def times(out, in_, c):
+        return either(out, v_ts(out, in_, c, A.mult), s_act(out, in_, ACT.Copy, scale=c))
+
+    def line(out, in_, c, d):
+        return either(out, v_ts(out, in_, c, A.mult, d, A.add), s_act(out, in_, ACT.Identity, bias=d, scale=c))
+
+    def mask(out, in_, h):
+        return either(out, v_ts(out, in_, R("MK", h, h + 1), A.mult), s_act(out, in_, ACT.Copy, scale=col(CH if h else CE)))
+
+    def tt(out, in0, in1, op):
+        i, rd = opnd(in0)
+        return call({"v": (lambda e: e.tensor_tensor(ap(out), i, ap(in1), op), cost(out, in0, 2.0))}, rd + [in1], [out])
+
+    def scan(out, d0, d1, init, op0, op1):
+        a, r = scal(init)
+        return call({"v": (lambda e: e.tensor_tensor_scan(ap(out), ap(d0), ap(d1), a, op0, op1), cost(out, d0, None, [d1] + r))}, [d0, d1] + r, [out])
+
+    def tr(out, in_):
+        return call({"v": (lambda e: e.transpose(ap(out), ap(in_)), cost(out, in_, None))}, [in_], [out])
+
+    def g_iota(out, pat, base, cm=0):
+        c = 0.14 + 2 * CYC * size(out) + LAG
+        if SCRATCH[out[0]][2] == I32:
+            return (lambda e: e.iota(ap(out), pat, base, cm), c)
+        return (lambda e: e.iota(ap(out), pat, base, cm, allow_small_or_imprecise_dtypes=True), c)
+
+    def iota(out, pat, base, cm=0):
+        return call({"g": g_iota(out, pat, base, cm)}, [], [out])
+
+    def mset(out, val, plain=False):
+        opts = {"v": (lambda e: e.memset(ap(out), val), cost(out, out, None))}
+        if val == int(val) and abs(val) <= 1000 and not plain:
+            opts["g"] = g_iota(out, [[0, size(out)]], int(val))
+        return call(opts, [], [out])
+
+    def scatter(win, off, src):
+        return call({"v": (lambda e: e.tensor_copy(ap(win).indirect(ap(off)), ap(src)), 0.06 + SCA * CYC * size(src))}, [off, src], [win])
 
     def quant(qc, qs, a, n, tile):
         oc, os_ = R(qc, a, a + n), R(qs, a, a + n)
-        return emit("v", lambda e: e.quantize_mx(ap(oc), ap(os_), ap(tile)), [tile], [oc, os_])
+        return call({"v": (lambda e: e.quantize_mx(ap(oc), ap(os_), ap(tile)), 0.013 + 0.00097 * n)}, [tile], [oc, os_])
 
     def mm(bk, n, lc, ls, la, rc, rs, ra):
         o = R("PS", 512 * bk, 512 * bk + n)
         rr = [R(lc, la, la + 128), R(ls, la, la + 128), R(rc, ra, ra + n), R(rs, ra, ra + n)]
-        return emit("p", lambda e: e.matmul_mx(ap(o), ap(rr[0]), ap(rr[1]), ap(rr[2]), ap(rr[3]), True, True), rr, [o])
+        return call({"p": (lambda e: e.matmul_mx(ap(o), ap(rr[0]), ap(rr[1]), ap(rr[2]), ap(rr[3]), True, True), 0.0007 * (n + 16))}, rr, [o])
 
-    def nextbank():
-        bank[0] = (bank[0] + 1) % 8
-        return bank[0]
-
-    def iota(out, pat, base, cm=0):
-        o = ap(out)
-        if SCRATCH[out[0]][2] == I32:
-            return emit("g", lambda e: e.iota(o, pat, base, cm), [], [out])
-        return emit("g", lambda e: e.iota(o, pat, base, cm, allow_small_or_imprecise_dtypes=True), [], [out])
-
-    def asel(out, in_, pat, op, fill, base, cm, quarter=None):
-        if quarter is None:
-            o, i = ap(out), ap(in_)
-        else:
-            o = T[out[0]][32 * quarter:32 * quarter + 32, out[1]:out[2]]
-            i = T[in_[0]][32 * quarter:32 * quarter + 32, in_[1]:in_[2]]
-        return emit("g", lambda e: e.affine_select(o, i, pat, op, fill, base, cm), [in_], [out])
-
-    def dma(q, out, in_, reads, writes):
-        return emit(q, lambda e: e.dma_start(out, in_), reads, writes, dma=True)
+    def dma(qs, out, in_, reads, writes):
+        return call({q: (lambda e: e.dma_start(out, in_), 0.1) for q in qs}, reads, writes, "dma", DMA)
 
     dma("y", T.X[:, 16:656], T.x[:, 0:640], [], [R("X", 16, 656)])
     dma("y", T.X[:, 656:1296], T.x[:, 640:1280], [], [R("X", 656, 1296)])
@@ -224,381 +290,330 @@ def rank_program(g, core, T, topo):
     dma("y", T.WS[:], T.ws[:], [], [R("WS")])
     dma("y", T.VT[:], T.v[:], [], [R("VT")])
 
-    p16 = [[0, 10], [1, 16]]
+    io = R("OLW", 160, 320)
+
+    def upto(n):
+        return R("OLW", 160, 160 + n)
+
+    def lf(c, n, s=1):
+        return R("LF", c, c + n, s)
+
     iota(R("PI", 0, 1), [[0, 1]], 0, 1)
-    iota(R("J40"), [[32, 5], [0, 4], [16, 2]], 0)
-    mset(R("X", 0, 16), 0.0)
-    mset(R("ONEB"), 1.0)
-    mset(R("BIGF"), 1.0e29)
-    for a in range(4):
-        asel(R("JM"), R("J40"), [[0, 5], [1, 4], [0, 2]], A.is_equal, -1000.0, -a, 0, quarter=a)
-    iota(R("KI", 30, 40), [[64, 5], [1, 2]], 0)
-    iota(R("FT0"), p16, 0)
-    iota(R("KI", 0, 10), [[16, 10]], 15)
-    iota(R("KI", 10, 20), [[4, 10]], 3)
-    asel(R("RS16"), R("ONEB"), p16, A.not_equal, 0.0, 0, 0)
-    asel(R("RT"), R("BIGF"), p16, A.not_equal, TINY, 0, 0)
-    iota(R("KK", 0, 2), [[256, 2]], 0)
-    iota(R("KK", 4, 8), [[4, 4]], 0)
-    iota(R("LA"), [[32, 10], [0, 16]], -159)
+    iota(R("J40"), [[32, 5], [0, 4], [16, 2]], 1000)
+    iota(R("A40"), [[0, 5], [1, 4], [0, 2]], 0)
+    iota(R("FT0"), [[0, 10], [1, 16]], 0)
+    iota(io, [[1, 160]], 0)
+    for name in ("X", "G", "AR"):
+        mset(R(name, 0, 16), 0.0, True)
+    mset(R("M", 4 * CUT - 256, 256), 0.0, True)
+    for r, val in ((R("RS16"), 1.0), (R("RS16", 0, 160, 16), 0.0), (R("RT"), 1.0e29), (R("RT", 0, 160, 16), TINY), (R("RS4"), 1.0), (R("RS4", 0, 64, 4), 0.0),
+                   (R("VAL"), 0.0), (R("ORS"), 0.0), (R("D0"), 0.0), (R("TH"), 0.0), (R("LM"), -1000.0), (lf(L_N, 24), 0.0),
+                   (R("ORK", 0, 320), FREE), (R("ORK", 320, 640), FREE), (R("ORK", 640, 960), FREE)):
+        mset(r, val)
     p0 = R("PI", 0, 1)
     ts(R("PI", C16, C16 + 1), p0, 15, A.bitwise_and)
     ts(R("PI", CH, CH + 1), p0, 4, A.logical_shift_right, 1, A.bitwise_and)
     ts(R("PI", CU, CU + 1), p0, 1, A.bitwise_and)
     ts(R("PI", C32, C32 + 1), p0, 31, A.bitwise_and)
     ts(R("PI", C4Q, C4Q + 1), p0, 2, A.logical_shift_right, 3, A.bitwise_and)
-    mset(R("OR"), 0.0)
-    cp(R("COL", 1, 6), R("PI", 1, 6))
-    mset(R("D0"), 0.0)
-    ts(R("MK", 0, 1), col(CH), -1.0, A.mult, 1.0, A.add)
+    ts(R("PI", CQ, CQ + 1), p0, 5, A.logical_shift_right)
+    cp(R("COL", 1, 7), R("PI", 1, 7))
+    line(R("MK", 0, 1), col(CH), -1.0, 1.0)
+    move(R("MK", 1, 2), col(CH))
+    line(col(CE), col(CH), -1.0, 1.0)
     tt(col(CNE), col(CU), col(CH), A.not_equal)
-    ts(col(CX16), col(C16), 16.0, A.mult)
-    ts(col(C64), col(C32), 2.0, A.mult)
-    ts(col(C2X), col(C16), 2.0, A.mult)
-    cp(R("MK", 1, 2), col(CH))
-    ts(col(CE), col(CH), -1.0, A.mult, 1.0, A.add)
-    ts(col(CT4), col(CNE), 336.0, A.mult, col(CX16), A.add)
-    mset(R("TH"), 0.0)
-    ts(R("JF"), R("JM"), col(C16), A.add)
-    ts(lst(L_X, 10), R("KI", 30, 40), col(C64), A.add)
-    ts(lst(L_PS, 40), R("JF"), 4.0, A.add, 0.0, A.max)
-    ts(lst(L_PK, 40), R("JF"), 164.0, A.add, 0.0, A.max)
-    act(R("J2"), R("JF"), ACT.Copy, scale=2.0)
-    ts(lst(L_PA, 40), R("J2"), 4.0, A.add, 0.0, A.max)
-    ts(lst(L_PR, 40), R("J2"), 5.0, A.add, 0.0, A.max)
+    times(col(CX16), col(C16), 16.0)
+    times(col(C64), col(C32), 2.0)
+    line(col(CM), col(C16), 2.0, -159.0)
+    line(col(CT), col(C16), 2.0, -160.0)
+    ts(R("JM"), R("A40"), col(CQ), A.is_equal)
+    line(R("J40"), R("J40"), 1.0, col(C16))
+    tt(R("JF"), R("J40"), R("JM"), A.mult)
+    for first, c, d in ((L_PS, 1.0, -996.0), (L_PK, 1.0, -836.0), (L_PA, 2.0, -1996.0), (L_PR, 2.0, -1995.0)):
+        act(lf(first, 40), R("JF"), ACT.Relu, bias=d, scale=c)
+    line(lf(L_XB, 10), upto(10), 32.0, col(C32))
+    line(lf(L_END, 10), upto(10), 16.0, 15.0)
+    cp(lst(0, L_PA), lf(0, L_PA))
+    line(lf(L_X, 10, 2), upto(5), 64.0, col(C64))
+    line(lf(L_X + 1, 9, 2), lf(L_X, 10, 2), 1.0, 1.0)
+    line(R("LT"), upto(4), 4.0, col(C4Q))
+    for k, (a, b) in enumerate(PIECES):
+        line(lf(L_LC + a // 16, (b - a) // 16), upto((b - a) // 16), 4.0, 3.0 + 32.0 * k)
+        ts(R("JM", 2 * k, 2 * k + 2), R("LT", 0, 2), (b - a) / 16.0 - 1.0, A.min)
+        line(lf(L_N + 2 * k, 2), R("JM", 2 * k, 2 * k + 2), 16.0, 15.0 + a)
+    for first, c, top, far in ((L_3G, CG0, 11.0, 208.0), (L_3G + 2, CG1, 7.0, 208.0), (L_3S, CS1, 9.0, 176.0)):
+        ts(col(c), col(C16), top, A.min, 16.0, A.mult)
+        line(lf(first, 1), col(CNE), far, col(c))
+    cp(lst(L_PA, 124), lf(L_PA, 124))
+    ts(R("M16"), R("FT0"), col(C16), A.is_equal)
+    ts(R("FT1"), R("FT0"), col(C16), A.is_ge, -2.0 ** -24, A.mult)
+    line(R("FT"), R("FT1"), 1.0, 1.0)
+    line(R("DM"), R("M16"), 1.0e29, FAR)
+    line(R("LM", 0, 160, 16), upto(10), 32.0, col(CM))
+    line(R("LM", 160, 320, 16), upto(10), 32.0, col(CT))
+    line(R("VS"), io, 2.0, -159.0)
+    line(R("JR", 0, 160), io, 2.0, -160.0)
+    line(R("JR", 160, 320), io, 1.0, -160.0)
 
-    def setup2():
-        ts(R("M16"), R("FT0"), col(C16), A.is_equal)
-        cp(lst(L_END, 20), R("KI", 0, 20))
-        ts(R("FT1"), R("FT0"), col(C16), A.is_ge, -2.0 ** -24, A.mult)
-        act(R("FT"), R("FT1"), ACT.Identity, bias=1.0)
+    def products(k, kind, qu, n, plist):
+        lo, hi = PIECES[k][0] // 32, PIECES[k][1] // 32
+        quant("QV" + kind, "SV" + kind, 64 * lo, 64 * (hi - lo), R("MV" + kind, 256 * lo, 256 * hi))
+        off = lst(plist + 8 * lo, 8 * (hi - lo))
+        oc, os_ = R("QS" + kind, 128 * lo, 128 * hi), R("SS" + kind, 128 * lo, 128 * hi)
+        wc, ws = R("QU" + qu, 0, n), R("SU" + qu, 0, n)
+        move(os_, (ws, off))
+        call({"v": (lambda e: e.tensor_copy(ap(oc).bitcast(dt.uint32), ap(wc).bitcast(dt.uint32).indirect(ap(off))), cost(oc, (wc, off), None))}, [wc, off], [oc])
+        for b in range(lo, hi):
+            bk = BANKS[k][b - lo + ("n" == kind)]
+            first = min(64 * b, 64 * hi - 128)
+            mm(bk, 128, "QS" + kind, "SS" + kind, 128 * b, "QV" + kind, "SV" + kind, first)
+            o = 512 * bk + 64 * b - first
+            move(R("Z" + kind, 64 * b, 64 * b + 64), R("PS", o, o + 64))
 
-    def setup3():
-        ts(R("LT"), R("KK", 4, 8), col(C4Q), A.add, 16.0, A.mult)
-        ts(lst(L_3G, 2), R("KK", 0, 2), col(CT4), A.add, 671.0, A.min)
+    def blocks(k, kind, e0):
+        for b in range(PIECES[k][0] // 32, PIECES[k][1] // 32):
+            for h in range(2):
+                mask(R("MV" + kind, 256 * b + 128 * h, 256 * b + 128 * h + 128), R("X", e0 + 128 * b, e0 + 128 * b + 128), h)
 
-    def setup3b():
-        ts(lst(L_N, 1), R("LT", 0, 1), 15.0, A.add, 159.0, A.min)
-        ts(lst(L_N + 2, 2), R("LT", 1, 3), 15.0, A.add, 159.0, A.min)
+    def pairs(k, kind, src, plist):
+        a, b = PIECES[k]
+        first = 0 if k == 0 else 4 + 2 * a
+        quant("QU" + kind, "SU" + kind, first, 4 + 2 * b - first, R(src, 4 * first, 16 + 8 * b))
+        for h in range(2):
+            for t in range(4):
+                mask(R("MV" + kind, 8 * a + 4 * h + t, 8 * b, 8), R(src, 20 + 8 * a + t, 16 + 8 * b, 8), h)
+        products(k, kind, kind, 4 + 2 * b, plist)
 
-    def setup4():
-        act(R("NEG0"), R("M16"), ACT.Identity, bias=FAR, scale=-FAR)
-        act(R("LB"), R("LA"), ACT.Identity, bias=col(C2X))
-        act(R("NEG"), R("NEG0"), ACT.Identity, bias=-TINY)
-        act(R("LB2"), R("LB"), ACT.Identity, bias=-1.0)
-        iota(R("IO"), [[1, 320]], -160)
-        asel(R("RS4"), R("ONEB", 0, 48), [[0, 12], [1, 4]], A.not_equal, 0.0, 0, 0)
-        asel(R("LM"), R("LB"), p16, A.is_equal, -1000.0, 0, 0)
-        asel(R("LS"), R("LB2"), p16, A.is_equal, -1000.0, 0, 0)
+    def diagonal(k, kind, first):
+        a, b = PIECES[k]
+        return (R("Z" + kind, 0, 2 * b), lst(first + a // 16, (b - a) // 16))
 
-    def gram(src, tile, qa, qn, plist, e0, step, plan, smid=None, smid2=None, vmid=None):
-        for what in plan.split():
-            if what == "q":
-                quant("QU", "SU", qa, qn, tile)
-                continue
-            h, t = "eo".index(what[1]), int(what[2])
-            o, i = R("MV", 4 * h + t, 1280, 8), R(src, e0 + t, e0 + 160 * step, step)
-            if what[0] == "s":
-                act(o, i, ACT.Copy, scale=col(CH if h else CE))
-            else:
-                ts(o, i, R("MK", h, h + 1), A.mult)
-        quant("QV", "SV", 0, 320, R("MV"))
-        banks = []
-        for lo, hi in ((0, 2), (2, 5)):
-            off = lst(plist + 8 * lo, 8 * (hi - lo))
-            oc, os_ = R("QS", 128 * lo, 128 * hi), R("SS", 128 * lo, 128 * hi)
-            emit("s", lambda e: e.activation(ap(os_), T.SU[:, 0:324].indirect(ap(off)), ACT.Copy), [R("SU"), off], [os_])
-            emit("v", lambda e: e.tensor_copy(ap(oc).bitcast(dt.uint32), T.QU[:, 0:324].bitcast(dt.uint32).indirect(ap(off))), [R("QU"), off], [oc])
-            for b in range(lo, hi):
-                bk = nextbank()
-                banks.append(bk)
-                mm(bk, 128, "QS", "SS", 128 * b, "QV", "SV", min(64 * b, 192))
-            if lo == 0 and smid is not None:
-                smid()
-        if smid2 is not None:
-            smid2()
-        for b in range(5):
-            o = 512 * banks[b] + (64 if b == 4 else 0)
-            act(R("Z", 64 * b, 64 * b + 64), R("PS", o, o + 64), ACT.Copy)
-        if vmid is not None:
-            vmid()
+    def ends(buf, o, k):
+        a, b = PIECES[k]
+        return (R(buf, o, o + b), lst(L_END + a // 16, (b - a) // 16))
 
-    zpart = [((R("Z", 0, 128), lst(L_X, 4)), 0, 64), ((R("Z"), lst(L_X + 4, 6)), 64, 160), ((R("Z"), lst(L_X, 10)), 0, 160)]
+    def row(half, a, b):
+        return R("DS", 2 * a + 1, 2 * b + 1, 2) if half == 0 else R("UU", 160 + a, 160 + b)
 
-    def zm(k, other="M16", op=A.mult, out="ZM"):
-        z, a, b = zpart[k]
-        tt(R(out, a, b), z, R(other, a, b), op)
+    def sizes(k, half, kind, first, other, op):
+        o = 160 * half
+        a, b = PIECES[k]
+        zm, zs, eb, gt = [R(n, o + a, o + b) for n in ("ZM", "ZS", "EB", "GT")]
+        tt(zm, diagonal(k, kind, first), R(other, a, b), op)
+        tr(gt, zm)
+        scan(R("GS", o + a, o + b), R("RT", a, b), gt, 1.0, A.min, A.max)
+        scan(zs, R("RT", a, b), zm, 1.0, A.min, A.max)
+        move(eb, ends("ZS", o, k))
+        tr(row(half, a, b), eb)
+        times(row(half, 160 + a, 160 + b), row(half, a, b), BELOW)
+        tt(R("Y", o + a, o + b), ends("GS", o, k), R("FT", a, b), A.mult)
+        tt(R("DC", o + a, o + b), row(half, a, b), R("Y", o + a, o + b), A.is_le)
+        scan(R("DG", o + a, o + b), R("RS16", a, b), R("DC", o + a, o + b), 0.0, A.mult, A.add)
 
-    def zs(k, op=A.add):
-        z, a, b = zpart[k]
-        scan(R("ZS", a, b), R("RS16", a, b), R("ZM", a, b), 0.0, A.mult, op)
-
-    def gt(k, src="ZM", out="GT"):
-        z, a, b = zpart[k]
-        tr(R(out, a, b), R(src, a, b))
-
-    def eb(k):
-        z, a, b = zpart[k]
-        ts(R("EB", a, b), (R("ZS", 0, b), lst(L_END + a // 16, (b - a) // 16)), TINY, A.max)
-
-    def gs(k, half):
-        z, a, b = zpart[k]
-        scan(R("GS", 160 * half + a, 160 * half + b), R("RT", a, b), R("GT", a, b), 1.0, A.min, A.max)
-
-    def row(k, half):
-        z, a, b = zpart[k]
-        tr(R("U2", a, b) if half == 0 else R("U", 192 + a, 192 + b), R("EB", a, b))
-
-    def below(half):
-        if half == 1:
-            ts(R("U", 512, 672), R("U", 192, 352), BELOW, A.mult)
-            return
-        ts(R("U2", 160, 320), R("U2", 0, 160), BELOW, A.mult)
-        act(R("U", 352, 512), R("U2", 0, 160), ACT.Copy, scale=BELOW)
-        act(R("U", 32, 192), R("U2", 0, 160), ACT.Copy)
-
-    def sizes(half):
-        zs(2, A.max)
-        gt(2)
-        eb(2)
-        gs(2, half)
-        row(2, half)
-
-    def diag(half):
-        return [lambda: tt(R("Y"), (R("GS", 160 * half, 160 * half + 160), lst(L_END, 10)), R("FT"), A.mult),
-                lambda: tt(R("DC"), R("U", 192, 352) if half else R("U2", 0, 160), R("Y"), A.is_le),
-                lambda: scan(R("DG", 160 * half, 160 * half + 160), R("RS16"), R("DC"), 0.0, A.mult, A.add)]
-
-    def gcol(e):
-        return R("GS", 16 * e + 15, 16 * e + 16)
-
-    def vsteps(steps, lo=0, hi=None, between=()):
-        def fin(k):
-            buf, a, n, e, init = steps[k]
-            h = n // 2
-            scan(R("SO", 152 * k, 152 * k + h), R("CB", 304 * k, 304 * k + h), R("CB", 304 * k + h, 304 * k + n), init, A.add, A.add)
-        hi = len(steps) if hi is None else hi
-        between = list(between)
-        nxt = lo
-        for k in range(lo, hi):
-            buf, a, n, e, init = steps[k]
-            ts(R("CB", 304 * k, 304 * k + n), R(buf, a, a + n), gcol(e), A.is_lt, 0.5, A.subtract)
-            if between:
-                between.pop(0)()
-            else:
-                for _ in range(2):
-                    if nxt < k:
-                        fin(nxt)
-                        nxt += 1
-        for k in range(nxt, hi):
-            fin(k)
-
-    def ssteps(steps):
-        def fin(k):
-            buf, a, n, e, sb, sa, sn, acc = steps[k]
-            act(R(sb, sa, sa + sn), R(sb, sa, sa + sn), ACT.Relu, accum=acc)
-        for k, (buf, a, n, e, sb, sa, sn, acc) in enumerate(steps):
-            act(R(sb, sa, sa + n), R(buf, a, a + n), ACT.Sign, bias=gcol(e), scale=-1.0)
-            if k >= LAGS:
-                fin(k - LAGS)
-        for k in range(max(0, len(steps) - LAGS), len(steps)):
-            fin(k)
-
-    def stayers_s(lo, hi):
-        ssteps([("U2", 16 * m + 16, 144, m, "SB2", 144 * m, 144, R("SB", W * m + 305, W * m + 306)) for m in range(lo, hi)])
-
-    def dgc(e):
-        return R("DG", 16 * e + 15, 16 * e + 16)
-
-    def planes(a, n):
+    def fresh(k):
+        a, b = PIECES[k]
+        blocks(k, "d", 656)
+        products(k, "d", "d", 164 + b, L_PK)
         for t in range(4):
-            act(R("XP", 320 * t + a, 320 * t + a + n), R("X", 16 + 4 * a + t, 16 + 4 * (a + n), 4), ACT.Copy)
+            move(R("XP", 320 * t + 160 + a, 320 * t + 160 + b), R("X", 656 + 4 * a + t, 656 + 4 * b, 4))
+        sizes(k, 1, "d", L_XB, "M16", A.mult)
 
-    def scatter(lo, hi):
-        win, off, src = R("OR", 16, 336), R("OFFS", lo, hi), R("IO", 16 * lo, 16 * hi)
-        emit("v", lambda e: e.tensor_copy(ap(win).indirect(ap(off)), ap(src)), [off, src], [win])
+    def count(half, ns):
+        e0 = 10 * half
+        n = 144 + 160 * half
+        move(R("SB", W * e0 + n, W * (e0 + ns), W), R("DG", 16 * e0 + 15, 16 * (e0 + ns), 16))
+        for m in range(10):
+            e = e0 + m
+            g_ = R("GS", 16 * e + 15, 16 * e + 16)
+            o = 0
+            for r in ([row(0, 160, 320)] if half else []) + [row(half, 16 * m + 16, 16 * m + 160)]:
+                if m < ns:
+                    act(R("SB", W * e + o, W * e + o + size(r)), r, ACT.Sign, bias=g_, scale=-1.0)
+                else:
+                    ts(R("CB", 304 * e + o, 304 * e + o + size(r)), r, g_, A.is_lt, 0.5, A.subtract)
+                o += size(r)
+            if m < ns:
+                act(R("SB", W * e, W * e + n + 1), R("SB", W * e, W * e + n + 1), ACT.Relu, accum=R("ACC", e, e + 1))
+            else:
+                h = n // 2
+                scan(R("SO", 152 * e, 152 * e + h), R("CB", 304 * e, 304 * e + h), R("CB", 304 * e + h, 304 * e + n), R("DG", 16 * e + 15, 16 * e + 16), A.add, A.add)
+        sgn, top = (1.0, 0.0) if half else (-1.0, 159.0)
+        ts(R("OFFS", e0, e0 + ns), R("ACC", e0, e0 + ns), sgn, A.mult, top, A.add)
+        ts(R("OFFS", e0 + ns, e0 + 10), R("SO", 152 * (e0 + ns) + n // 2 - 1, 152 * (e0 + 10), 152), sgn, A.mult, top + sgn * (n // 2), A.add)
+
+    def sort_stayers(rnd):
+        count(0, NS[rnd])
+        scatter(R("ORS", 16, 176), R("OFFS", 0, 10), R("VS"))
+        tr(R("TS", 0, 160), R("ORS", 16, 176))
+        tr(R("TS", 160, 352), R("ORS"))
+        where = (R("TS"), lst(L_3S, 1))
+        ts(R("OS", 0, 16), where, 160.0, A.add)
+        move(R("UU", 0, 160), (R("DS", 0, 320), R("OS", 0, 10)))
+        for t in range(4):
+            ts(R("OS", 16 * t + 16, 16 * t + 32), where, 4.0, A.mult, 656.0 + t, A.add)
+            move(R("XP", 320 * t, 320 * t + 160), (R("AR"), R("OS", 16 * t + 16, 16 * t + 26)))
+        if rnd == 2:
+            scatter(R("OLW", 0, 160), R("OFFS", 0, 10), R("JR", 160, 320))
 
     def order(rnd):
-        ns = NS0 if rnd == 0 else NS
-        ssteps([("U", 192, 160, e, "SB", W * e + 144, 162, R("ACC", e, e + 1)) for e in range(10)])
-        d = diag(1)
-        d[0]()
-        below(1)
-        d[1]()
-        bt = [d[2]]
-        if ns > 10:
-            def longs():
-                cp(R("SB", W * 10 + 304, W * ns, W), R("DG", 175, 16 * ns, 16))
-                ssteps([("U", 48 + 16 * e, 304, e, "SB", W * e, 305, R("ACC", e, e + 1)) for e in range(10, ns)])
-            bt.append(longs)
-        vsteps([("U", 48 + 16 * e, 304, e, dgc(e)) for e in range(ns, 20)], between=bt)
-        cp(R("OFFS", 0, 10), R("ACC", 0, 10))
-        ts(R("OFFS", ns, 20), R("SO", 151, 152 * (20 - ns), 152), 152.0, A.add)
-        scatter(0, 10)
-        if ns > 10:
-            cp(R("OFFS", 10, ns), R("ACC", 10, ns))
-        if rnd == 0:
-            planes(0, 320)
-        else:
-            planes(160, 160)
-        scatter(10, 20)
-        tr(R("TT", 0, 320), R("OR", 16, 336))
-        tr(R("TT", 320, 672), R("OR"))
-        ts(R("OG"), (R("TT"), lst(L_3G, 2)), 160.0, A.add)
-        for t, q in ((0, "s"), (2, "v"), (1, "s"), (3, "v")):
-            gat(q, R("G", t, 1280, 4), R("XP", 320 * t, 320 * t + 320), R("OG", 0, 20))
+        count(1, NK[rnd])
+        for p, q in ((NK[rnd], 10), (0, NK[rnd])):
+            scatter(R("ORK", 320 * rnd, 320 * rnd + 320), R("OFFS", 10 + p, 10 + q), R("OLW", 160 + 16 * p, 160 + 16 * q))
+        for k, (a, b) in enumerate(PIECES):
+            p, q = (0, 2 * b + 16) if k == 0 else (2 * a + 16, 320)
+            o = R("ORK", 320 * rnd + p, 320 * rnd + q)
+            ts(R("FL", p, q), o, -100.0, A.is_lt, -0.5, A.mult)
+            scan(R("CU", p, q), R("FL", p, q), R("FL", p, q), R("CU", p - 1, p) if k else 0.0, A.add, A.add)
+            scan(R("VAL", 16 + p, 16 + q), R("CU", p, q), o, 0.0, A.min, A.max)
+            n = 2 * (b - a)
+            tr(R("TT", 448 * k, 448 * k + n), R("VAL", 16 + 2 * a, 16 + 2 * b))
+            tr(R("TT", 448 * k + 192, 448 * k + 224 + n), R("VAL", 2 * a, 32 + 2 * b))
+            ts(R("OG", 16 * k, 16 * k + 16), (R("TT", 448 * k, 448 * k + 224 + n), lst(L_3G + 2 * k, 1)), 160.0, A.add)
+        for k, (a, b) in enumerate(PIECES):
+            og = R("OG", 16 * k, 16 * k + (b - a) // 8)
+            for t in range(4):
+                move(R("G", 16 + 8 * a + t, 16 + 8 * b, 4), (R("XP", 320 * t, 320 * t + 320), og))
+            move(R("DS", 2 * a, 2 * b), (R("UU", 0, 320), og))
 
-    def thresholds():
-        tr(R("TD"), R("DS", 0, 320, 2))
-        ts(R("TH", 0, 40, 4), R("TD", 0, 160, 16), 0.75, A.mult)
-        ts(R("TH", 1, 40, 4), R("TD", 0, 160, 16), 0.25, A.mult)
-        ts(R("TH", 2, 40, 4), R("TD", 0, 160, 16), 0.75, A.mult, -BELOW, A.mult)
-        ts(R("TH", 3, 40, 4), R("TD", 0, 160, 16), 0.25, A.mult, -BELOW, A.mult)
-        zm(0)
-        tt(R("DA"), R("TD"), R("NEG"), A.add)
-        zs(0)
-
-    def rem(k, t):
-        z, a, b = zpart[k]
-        scan(R("AR", 8 * a + t, 8 * b, 4), R("D0", 2 * a, 2 * b), R("G", 8 * a + t, 8 * b, 4), 0.0, A.mult, A.add)
-
-    def emid():
-        zm(0, "DA", A.is_lt, "SD")
-        gt(0, "SD", "ST")
-
-    def offsets(out, pos, which):
-        for t in which:
-            ts(R(out, 16 * t, 16 * t + 10), R(pos, 15, 160, 16), 4.0, A.mult, 640.0 + t, A.add)
-
-    def finish(half):
-        a = 160 * half
-        quant("QF", "SF", a, 160, R("X", 16 + 4 * a, 16 + 4 * a + 640))
-        bk = nextbank()
-        mm(bk, 160, "QW", "SW", 0, "QF", "SF", a)
-        dma("y", T.oc[:, 4 * a:4 * a + 640], T.QF[:, a:a + 160].bitcast(dt.uint8), [R("QF", a, a + 160)], [])
-        for k in range(4):
-            dma("s" if (half == 1 and k >= 2) else "y", T.osc[4 * k:4 * k + 4, a:a + 160], T.SF[32 * k:32 * k + 4, a:a + 160], [R("SF", a, a + 160)], [])
-        cp(R("YO", a, a + 160), R("PS", 512 * bk, 512 * bk + 160))
-        dma("s" if half == 1 else "y", T.y[:, a:a + 160], T.YO[:, a:a + 160], [R("YO", a, a + 160)], [])
-
-    gram("X", R("X", 0, 656), 0, 164, L_PS, 16, 4, PLAN_X, vmid=setup2)
-    setup4()
-    zm(2)
-    sizes(0)
-    setup3()
-    below(0)
-    nsent = 0
-    late = [None]
-    for rnd in range(3):
-        if rnd == 0:
-            def vmid0():
-                d = diag(0)
-                d[0]()
-                setup3b()
-                d[1]()
-                zm(0)
-                d[2]()
-                zs(0)
-                gt(0)
-                cp(R("SB", 304, W * 10, W), R("DG", 15, 160, 16))
-            gram("X", R("X", 656, 1296), 164, 160, L_PK, 656, 4, PLAN_X, smid2=lambda: stayers_s(0, 2), vmid=vmid0)
-            stayers_s(2, 10)
-        else:
-            gram("X", R("X", 656, 1296), 164, 160, L_PK, 656, 4, PLAN_K, vmid=late[0])
-        zm(1)
-        eb(0)
-        gs(0, 1)
-        zs(1)
-        gt(1)
-        row(0, 1)
-        eb(1)
-        gs(1, 1)
-        row(1, 1)
-        order(rnd)
-        gram("G", R("G"), 4, 320, L_PA, 4, 8, PLAN_N, smid=lambda: gat("s", R("DS"), R("U", 32, 352), R("OG", 0, 20)), vmid=thresholds)
-        if rnd == 2:
-            act(R("OLF"), R("OR", 16, 336), ACT.Identity, bias=160.0)
-            dma("y", T.ol[:], T.OLF[0:128:16, :], [R("OLF")], [])
-        zm(1)
-        tt(R("CMP", 0, 16), (R("ZS", 0, 64), lst(L_N, 1)), R("TH", 0, 16), A.is_ge)
-        zs(1)
-        scan(R("CS", 0, 16), R("RS4", 0, 16), R("CMP", 0, 16), 0.0, A.mult, A.add)
-        tt(R("CMP", 16, 48), (R("ZS"), lst(L_N + 2, 2)), R("TH", 16, 48), A.is_ge)
-        ts(R("EC", 0, 64), (R("CS", 0, 16), lst(L_LC, 4)), -0.5, A.mult, 1.0, A.add)
-        scan(R("CS", 16, 48), R("RS4", 16, 48), R("CMP", 16, 48), 0.0, A.mult, A.add)
-        tr(R("D0", 1, 128, 2), R("EC", 0, 64))
-        ts(R("EC", 64, 160), (R("CS"), lst(L_LC + 4, 6)), -0.5, A.mult, 1.0, A.add)
-        rem(0, 0)
-        rem(0, 1)
-        tr(R("D0", 129, 320, 2), R("EC", 64, 160))
-        rem(0, 2)
-        rem(0, 3)
+    def reduce(k):
+        a, b = PIECES[k]
+        pairs(k, "n", "G", L_PA)
+        tr(R("TD", a, b), R("DS", 2 * a, 2 * b, 2))
+        c0, c1, th = 32 * k, 32 * k + 16 * ((b - a + 63) // 64), 32 * k + (b - a) // 4
+        for i, c in enumerate((0.75, 0.25)):
+            times(R("TH", c0 + i, th, 4), R("TD", a, b, 16), c)
+            times(R("TH", c0 + i + 2, th, 4), R("TH", c0 + i, th, 4), -BELOW)
+        scan(R("DA", a, b), R("TD", a, b), R("DM", a, b), FAR, A.max, A.min)
+        zm, zs = R("ZM", 320 + a, 320 + b), R("ZS", 320 + a, 320 + b)
+        tt(zm, diagonal(k, "n", L_X), R("M16", a, b), A.mult)
+        scan(zs, R("RS16", a, b), zm, 0.0, A.mult, A.add)
+        tt(R("CMP", c0, c1), (R("ZS", 320, 320 + b), lst(L_N + 2 * k, (c1 - c0) // 16)), R("TH", c0, c1), A.is_ge)
+        scan(R("CS", c0, c1), R("RS4", c0, c1), R("CMP", c0, c1), 0.0, A.mult, A.add)
+        line(R("EC", a, b), (R("CS", 0, c1), lst(L_LC + a // 16, (b - a) // 16)), -0.5, 1.0)
+        tr(R("D0", 2 * a + 1, 2 * b, 2), R("EC", a, b))
         for t in range(4):
-            rem(1, t)
-        gram("AR", R("AR"), 4, 320, L_PR, 4, 8, PLAN_E, vmid=emid)
-        zm(1, "DA", A.is_lt, "SD")
-        gt(1, "SD", "ST")
-        scan(R("PM"), R("LM"), R("ST"), -1000.0, A.max, A.subtract)
-        scan(R("PT"), R("LS"), R("ST"), -1000.0, A.max, A.add)
-        offsets("OM", "PM", (0, 2, 1, 3))
-        offsets("OS", "PT", (0,))
-        for t, q in ((0, "s"), (2, "v"), (1, "s"), (3, "v")):
-            gat(q, R("M", t, 640, 4), R("AR"), R("OM", 16 * t, 16 * t + 10))
-        offsets("OS", "PT", (1, 2))
-        tq = quant("QM%d" % rnd, "SM%d" % rnd, 0, 160, R("M"))
+            scan(R("AR", 16 + 8 * a + t, 16 + 8 * b, 4), R("D0", 2 * a, 2 * b), R("G", 16 + 8 * a + t, 16 + 8 * b, 4), 0.0, A.mult, A.add)
+        pairs(k, "e", "AR", L_PR)
+        tt(R("SD", a, b), diagonal(k, "e", L_X), R("DA", a, b), A.is_lt)
+        tr(R("ST", a, b), R("SD", a, b))
+        scan(R("PM", a, b), R("LM", a, b), R("ST", a, b), -1000.0, A.max, A.subtract)
+        for t in range(4):
+            om = R("OM", 16 * t + a // 16, 16 * t + b // 16)
+            ts(om, R("PM", a + 15, b, 16), 4.0, A.mult, 656.0 + t, A.add)
+            move(R("M", 256 + 4 * a + t, 256 + 4 * b, 4), (R("AR", 0, 16 + 8 * b), om))
+
+    nsent = [0]
+
+    def hand_on(rnd, k):
+        a, b = PIECES[k]
+        n, o, to = b - a, 256 * rnd + 128 * k + 128, 128 + 160 * rnd + a
+        quant("QM", "SM", o - 128, 128, R("M", 4 * b - 256, 4 * b + 256))
         dst = T.cores[(rank + STEP[rnd]) % len(T.cores)]
-        rid, pid, _ = topo.addr(dst)
-        mask = topo.mask(core, dst)
-        ne = len(topo.engines(core, dst))
-        wait("g", tq)
-        g.remote_dma(T["LC%d" % rnd][:].bitcast(dt.uint8), T["QM%d" % rnd][:].bitcast(dt.uint8), T.sem["arr%d" % rnd], T.sem.sent, pid, rid, mask)
-        g.remote_dma(T["LS%d" % rnd][:], T["SM%d" % rnd][:], T.sem["arr%d" % rnd], T.sem.sent, pid, rid, mask)
-        nsent += 2 * ne
-        if rnd < 2:
-            zm(2, "DA", A.min)
-            offsets("OS", "PT", (3,))
-            for t in (0, 1, 2):
-                gat("s", R("XP", 320 * t, 320 * t + 160), R("AR"), R("OS", 16 * t, 16 * t + 10))
-            sizes(0)
-            d = diag(0)
-            d[0]()
-            below(0)
-            d[1]()
-            stayers_s(0, NSS)
-            steps = [("U2", 16 * m + 16, 144, m, 0.0) for m in range(NSS, 10)]
-            vsteps(steps, 0, len(steps) - NLATE, between=[lambda: None, d[2]])
-
-            def rest(steps=steps):
-                vsteps(steps, len(steps) - NLATE, len(steps), between=[lambda: zm(0)])
-                cp(R("SB", 304, W * 10, W), R("DG", 15, 160, 16))
-                zs(0)
-                gt(0)
-                ts(R("SB", W * NSS + 305, W * 10, W), R("SO", 71, 152 * (10 - NSS), 152), 72.0, A.add)
-            late[0] = rest
-            gat("s", R("XP", 960, 1120), R("AR"), R("OS", 48, 58))
-        else:
-            offsets("OS", "PT", (3,))
-            for t, q in ((0, "s"), (2, "v"), (1, "s"), (3, "v")):
-                gat(q, R("X", 16 + t, 656, 4), R("AR"), R("OS", 16 * t, 16 * t + 10))
-            quant("QW", "SW", 0, 128, R("VT"))
-            finish(0)
         src = T.cores[(rank - STEP[rnd]) % len(T.cores)]
-        g.tensor.wait_ge(T.sem["arr%d" % rnd], 2 * len(topo.engines(src, core)))
-        banks = []
-        for b in range(4):
-            bk = nextbank()
-            banks.append(bk)
-            mm(bk, 160, "WC", "WS", 128 * b, "LC%d" % rnd, "LS%d" % rnd, 0)
-        for b in (0, 1, 2, 3):
-            o, i = R("X", 656 + b, 1296, 4), R("PS", 512 * banks[b], 512 * banks[b] + 160)
-            if b in (KV if rnd < 2 else (0, 2)):
-                ts(o, i, 0.03125, A.mult)
-            else:
-                act(o, i, ACT.Copy, scale=0.03125)
-    finish(1)
+        arr = "arr%d" % (2 * rnd + k)
 
-    g.wait_ge(T.sem.sent, nsent)
+        def calls(e):
+            rid, pid, _ = topo.addr(dst)
+            engines = topo.mask(core, dst)
+            e.remote_dma(T.LC[:, to:to + n].bitcast(dt.uint8), T.QM[:, o - n:o].bitcast(dt.uint8), T.sem[arr], T.sem.sent, pid, rid, engines)
+            e.remote_dma(T.LS[:, to:to + n], T.SM[:, o - n:o], T.sem[arr], T.sem.sent, pid, rid, engines)
+            nsent[0] += 2 * len(topo.engines(core, dst))
+        node = call({"g": (calls, 0.6 + ONCE * (rnd + k == 0))}, [R("QM", o - n, o), R("SM", o - n, o)], [R("LC", to, to + n), R("LS", to, to + n)], "remote", HOP)
+        node["tok"] = (arr, 2 * len(topo.engines(src, core)), {})
+
+    def layer(rnd, k):
+        a, b = PIECES[k]
+        for i in range(4):
+            bk = BANKS[k][i]
+            mm(bk, 128, "WC", "WS", 128 * i, "LC", "LS", 160 * rnd + b)
+            times(R("X", 656 + 4 * a + i, 656 + 4 * b, 4), R("PS", 512 * bk + 128 - (b - a), 512 * bk + 128), 0.03125)
+
+    def finish(a, b, o, bk):
+        n, m = b - a, max(b - a, 128)
+        quant("QF", "SF", o - m, m, R("X", 16 + 4 * (b - m), 16 + 4 * b))
+        mm(bk, m, "QW", "SW", 0, "QF", "SF", o - m)
+        dma("ys", T.oc[:, 4 * a:4 * b], T.QF[:, o - n:o].bitcast(dt.uint8), [R("QF", o - n, o)], [])
+        for k in range(4):
+            dma("ys", T.osc[4 * k:4 * k + 4, a:b], T.SF[32 * k:32 * k + 4, o - n:o], [R("SF", o - n, o)], [])
+        move(R("YO", a, b), R("PS", 512 * bk + m - n, 512 * bk + m))
+        dma("ys", T.y[:, a:b], T.YO[:, a:b], [R("YO", a, b)], [])
+
+    quant("QUd", "SUd", 0, 164, R("X", 0, 656))
+    quant("QUd", "SUd", 164, 160, R("X", 656, 1296))
+    quant("LC", "LS", 0, 128, R("X", 0, 512))
+    for k in range(2):
+        blocks(k, "e", 16)
+        products(k, "e", "d", 164, L_PS)
+        sizes(k, 0, "e", L_XB, "M16", A.mult)
+        fresh(k)
+    for t in range(4):
+        move(R("AR", 20 + t, 1296, 8), R("X", 16 + t, 656, 4))
+    for rnd in range(3):
+        sort_stayers(rnd)
+        order(rnd)
+        for k, (a, b) in enumerate(PIECES):
+            reduce(k)
+            hand_on(rnd, k)
+            if rnd < 2:
+                sizes(k, 0, "e", L_X, "DA", A.min)
+            layer(rnd, k)
+            if rnd < 2:
+                quant("QUd", "SUd", 36 + b, 128, R("X", 144 + 4 * b, 656 + 4 * b))
+                fresh(k)
+        if rnd < 2:
+            tt(R("FS"), R("DS", 1, 320, 2), R("DS", 0, 320, 2), A.is_lt)
+            scan(R("VS"), R("JR", 0, 160), R("FS"), -1000.0, A.max, A.add)
+    for k, (a, b) in enumerate(PIECES):
+        act(R("OLF", 2 * a, 2 * b), (R("OLW"), R("OG", 16 * k, 16 * k + (b - a) // 8)), ACT.Identity, bias=160.0)
+    dma("y", T.ol[:], T.OLF[0:128:16, :], [R("OLF")], [])
+    scan(R("PT"), R("LM", 160, 320), R("ST"), -1000.0, A.max, A.add)
+    for t in range(4):
+        ts(R("OS", 16 * t + 16, 16 * t + 26), R("PT", 15, 160, 16), 4.0, A.mult, 656.0 + t, A.add)
+        move(R("X", 16 + t, 656, 4), (R("AR"), R("OS", 16 * t + 16, 16 * t + 26)))
+    quant("QW", "SW", 0, 128, R("VT"))
+    finish(0, 160, 160, 0)
+    if TAIL:
+        finish(160, 160 + CUT, 288, 1)
+        finish(160 + CUT, 320, 416, 4)
+    else:
+        finish(160, 320, 320, 1)
+
+    done = {q: 0 for q in sem}
+    known = {q: {} for q in eng}
+    ndma = 0
+
+    def wait(q, tok):
+        if known[q].get(tok[0], 0) < tok[1]:
+            eng[q].wait_ge(T.sem[tok[0]], tok[1])
+            known[q][tok[0]] = tok[1]
+            for k, val in tok[2].items():
+                if known[q].get(k, 0) < val:
+                    known[q][k] = val
+
+    for n, q in plan(nodes):
+        need = {}
+        for p in n["deps"]:
+            tok = p["tok"]
+            if tok[0] not in need or need[tok[0]][1] < tok[1]:
+                need[tok[0]] = tok
+        for tok in sorted(need.values(), key=lambda tok: -len(tok[2])):
+            wait(q, tok)
+        if q == "g":
+            wait("g", ("cg", done["g"], {}))
+        ins = n["opts"][q][0](eng[q])
+        clock = dict(known[q])
+        if n["kind"] == "dma":
+            name = "d%d" % ndma
+            ndma += 1
+            ins.then_inc(T.sem[name], 16)
+            n["tok"] = (name, 16, clock)
+        elif n["kind"] == "op":
+            done[q] += 1
+            ins.then_inc(T.sem[sem[q]], 1)
+            n["tok"] = (sem[q], done[q], clock)
+
+    g.wait_ge(T.sem.sent, nsent[0])
     for q in ("v", "s", "p", "g"):
-        g.wait_ge(T.sem[sem[q]], count[q])
-    for i in range(ndma[0]):
+        g.wait_ge(T.sem[sem[q]], done[q])
+    for i in range(ndma):
         g.wait_ge(T.sem["d%d" % i], 16)

@@ -5,15 +5,17 @@ F, B, U16, I32, C4, U8 = "float32", "bfloat16", "uint16", "int32", "float8_e4m3f
 STEP = [1, 2, 1]
 CUT = 96
 W = 306
-NK = [6, 6, 6]
+NK = [4, 4, 4]
 NS = [6, 6, 6]
 TINY = 2.0 ** -100
 BELOW = 1.0 - 2.0 ** -24
 FAR = -1.0e25
-FREE = -200.0
-CYC, GAT, SCA, LAG, DMA, HOP, ONCE = 0.00092, 1.56, 3.5, 0.18, 1.8, 2.4, 2.0
-SPARE, TURNS, SHAKES, SEED = 0.7, 2, 2500, 1
+FREE = -0.5
+SMALL = 2.0 ** -40
+CYC, GAT, SCA, LAG, DMA, HOP, ONCE = 0.00088, 1.56, 3.5, 0.23, 1.8, 2.2, 2.0
+SPARE, TURNS, SHAKES, SEED, SLACK = 0.7, 2, 4000, 1, 0.06
 TAIL = 1
+LAG2, FAST, ROB = 0.16, 1.15, 0.35
 PLANNED = []
 LEN = []
 
@@ -27,10 +29,11 @@ SCRATCH = {
     "X": _sb(1296, B), "XP": _sb(1280, B), "G": _sb(1296, B), "AR": _sb(1296, B), "M": _sb(896, B), "VT": _sb(512, B),
     "WC": _sb(512, C4), "WS": _sb(512, U8), "QW": _sb(128, C4), "SW": _sb(128, U8), "QF": _sb(416, C4), "SF": _sb(416, U8),
     "QM": _sb(768, C4), "SM": _sb(768, U8), "LC": _sb(608, C4), "LS": _sb(608, U8),
-    "UU": _sb(480, F), "DS": _sb(640, F), "GS": _sb(320, F), "RT": _sb(160, F),
-    "ZM": _sb(480, F), "ZS": _sb(480, F), "EB": _sb(320, F), "GT": _sb(320, F), "Y": _sb(320, F), "DC": _sb(320, B), "DG": _sb(320, B),
+    "UU": _sb(480, F), "DS": _sb(640, F), "GS": _sb(328, F), "FD": _sb(160, F), "O4": _sb(64, F),
+    "ZN": _sb(320, F), "M64": _sb(64, F), "M640": _sb(64, F), "RS32": _sb(160, B), "LI": _sb(8, I32), "LT4": _sb(8, F),
+    "ZM": _sb(320, F), "ZS": _sb(328, F), "EB": _sb(328, F), "GT": _sb(320, F), "Y": _sb(328, F), "DC": _sb(320, B), "DG": _sb(320, B),
     "CB": _sb(20 * 304, B), "SO": _sb(20 * 152, B), "SB": _sb(20 * W, F), "ACC": _sb(20, F), "OFFS": _sb(20, U16),
-    "ORK": _sb(960, B), "FL": _sb(320, B), "CU": _sb(320, B), "VAL": _sb(352, B), "TT": _sb(896, B), "OG": _sb(32, U16),
+    "ORK": _sb(1056, B), "TK": _sb(896, B), "IOT": _sb(160, B), "VAL": _sb(352, B), "TT": _sb(896, B), "OG": _sb(32, U16),
     "ORS": _sb(192, B), "TS": _sb(352, B), "OS": _sb(96, U16), "FS": _sb(160, B), "VS": _sb(160, B), "OLW": _sb(320, B), "JR": _sb(320, B),
     "TD": _sb(160, F), "DA": _sb(160, F), "TH": _sb(64, F), "CMP": _sb(64, F), "CS": _sb(64, F), "EC": _sb(160, B), "D0": _sb(320, B),
     "SD": _sb(160, B), "ST": _sb(160, B), "PM": _sb(160, B), "PT": _sb(160, B), "OM": _sb(64, U16),
@@ -55,7 +58,7 @@ BANKS = ((0, 1, 2, 3), (4, 5, 6, 7))
 
 L_PS, L_PK, L_XB, L_END = 0, 40, 80, 90
 L_PA, L_PR, L_LC, L_X, L_N, L_3G, L_3S = 100, 140, 180, 190, 200, 204, 208
-C16, CH, CU, C32, C4Q, CQ, CE, CNE, CX16, C64, CM, CT, CG0, CG1, CS1 = range(1, 16)
+C16, CH, CU, C32, C4Q, CQ, CE, CNE, CX16, C64, CM, CT, CG0, CG1, CS1, CN = range(1, 17)
 
 
 def plan(nodes):
@@ -92,6 +95,16 @@ def plan(nodes):
             start[i], end[i], queue[i] = t, t + c + (lat[i] if early else 0.0), q
         return end, start, queue
 
+    def length(order):
+        end, start, queue = order
+        free = {q: 0.0 for q in "vspgy"}
+        late = [0.0] * num
+        for i in sorted(range(num), key=lambda i: start[i]):
+            t = max([late[p] + LAG2 for p in deps[i]] + [free[queue[i]]])
+            free[queue[i]] = t + FAST * (end[i] - start[i] - lat[i])
+            late[i] = free[queue[i]] + lat[i]
+        return (1.0 - ROB) * max(end) + ROB * max(late)
+
     def tighten(rank, lean):
         return fill(fill(rank, lean, deps, True)[0], lean, nxt, False)[0]
 
@@ -102,6 +115,7 @@ def plan(nodes):
     for _ in range(TURNS):
         rank = tighten(rank, lean)
     now = fill(rank, lean, deps, True)
+    best = length(now)
     rng = np.random.RandomState(SEED)
     for step in range(SHAKES):
         t0 = rng.uniform(0.0, max(now[0]))
@@ -117,8 +131,9 @@ def plan(nodes):
         if step % 4 == 0:
             r = tighten(r, l)
         new = fill(r, l, deps, True)
-        if max(new[0]) <= max(now[0]) + 0.03 * (1.0 - step / SHAKES):
-            rank, lean, now = r, l, new
+        span = length(new)
+        if span <= best + SLACK * (1.0 - step / SHAKES):
+            rank, lean, now, best = r, l, new, span
     PLANNED.extend((i, now[2][i]) for i in sorted(range(num), key=lambda i: (now[1][i], i)))
     LEN.append(max(now[0]))
     return plan(nodes)
@@ -245,11 +260,15 @@ def rank_program(g, core, T, topo):
 
     def tt(out, in0, in1, op):
         i, rd = opnd(in0)
-        return call({"v": (lambda e: e.tensor_tensor(ap(out), i, ap(in1), op), cost(out, in0, 2.0))}, rd + [in1], [out])
+        return call({"v": (lambda e: e.tensor_tensor(ap(out), i, ap(in1), op), cost(out, in0, 1.0 if in0[0] == "PS" else 2.0))}, rd + [in1], [out])
+
+    def v_scan(out, d0, d1, init, op0, op1):
+        a, r = scal(init)
+        return (lambda e: e.tensor_tensor_scan(ap(out), ap(d0), ap(d1), a, op0, op1), cost(out, d0, None, [d1] + r)), [d0, d1] + r
 
     def scan(out, d0, d1, init, op0, op1):
-        a, r = scal(init)
-        return call({"v": (lambda e: e.tensor_tensor_scan(ap(out), ap(d0), ap(d1), a, op0, op1), cost(out, d0, None, [d1] + r))}, [d0, d1] + r, [out])
+        o, rd = v_scan(out, d0, d1, init, op0, op1)
+        return call({"v": o}, rd, [out])
 
     def tr(out, in_):
         return call({"v": (lambda e: e.transpose(ap(out), ap(in_)), cost(out, in_, None))}, [in_], [out])
@@ -306,9 +325,9 @@ def rank_program(g, core, T, topo):
     for name in ("X", "G", "AR"):
         mset(R(name, 0, 16), 0.0, True)
     mset(R("M", 4 * CUT - 256, 256), 0.0, True)
-    for r, val in ((R("RS16"), 1.0), (R("RS16", 0, 160, 16), 0.0), (R("RT"), 1.0e29), (R("RT", 0, 160, 16), TINY), (R("RS4"), 1.0), (R("RS4", 0, 64, 4), 0.0),
+    for r, val in ((R("RS16"), 1.0), (R("RS16", 0, 160, 16), 0.0), (R("RS4"), 1.0), (R("RS4", 0, 64, 4), 0.0),
                    (R("VAL"), 0.0), (R("ORS"), 0.0), (R("D0"), 0.0), (R("TH"), 0.0), (R("LM"), -1000.0), (lf(L_N, 24), 0.0),
-                   (R("ORK", 0, 320), FREE), (R("ORK", 320, 640), FREE), (R("ORK", 640, 960), FREE)):
+                   (R("ORK", 0, 352), FREE), (R("ORK", 352, 704), FREE), (R("ORK", 704, 1056), FREE)):
         mset(r, val)
     p0 = R("PI", 0, 1)
     ts(R("PI", C16, C16 + 1), p0, 15, A.bitwise_and)
@@ -340,14 +359,27 @@ def rank_program(g, core, T, topo):
     for k, (a, b) in enumerate(PIECES):
         line(lf(L_LC + a // 16, (b - a) // 16), upto((b - a) // 16), 4.0, 3.0 + 32.0 * k)
         ts(R("JM", 2 * k, 2 * k + 2), R("LT", 0, 2), (b - a) / 16.0 - 1.0, A.min)
-        line(lf(L_N + 2 * k, 2), R("JM", 2 * k, 2 * k + 2), 16.0, 15.0 + a)
+        cp(R("LI", 2 * k, 2 * k + 2), R("JM", 2 * k, 2 * k + 2))
+        ts(R("LI", 4 + 2 * k, 6 + 2 * k), R("LI", 2 * k, 2 * k + 2), 1, A.bitwise_and)
+        cp(R("LT4", 2 * k, 2 * k + 2), R("LI", 4 + 2 * k, 6 + 2 * k))
+        line(R("LT4", 4 + 2 * k, 6 + 2 * k), R("JM", 2 * k, 2 * k + 2), 16.0, 31.0 + a)
+        times(R("LT4", 2 * k, 2 * k + 2), R("LT4", 2 * k, 2 * k + 2), 144.0)
+        tt(lf(L_N + 2 * k, 2), R("LT4", 2 * k, 2 * k + 2), R("LT4", 4 + 2 * k, 6 + 2 * k), A.add)
     for first, c, top, far in ((L_3G, CG0, 11.0, 208.0), (L_3G + 2, CG1, 7.0, 208.0), (L_3S, CS1, 9.0, 176.0)):
         ts(col(c), col(C16), top, A.min, 16.0, A.mult)
         line(lf(first, 1), col(CNE), far, col(c))
     cp(lst(L_PA, 124), lf(L_PA, 124))
     ts(R("M16"), R("FT0"), col(C16), A.is_equal)
-    ts(R("FT1"), R("FT0"), col(C16), A.is_ge, -2.0 ** -24, A.mult)
+    iota(R("M640"), [[1, 32], [0, 2]], 0)
+    ts(R("M64"), R("M640"), col(C32), A.is_equal)
+    mset(R("RS32"), 1.0)
+    mset(R("RS32", 0, 160, 32), 0.0)
+    mset(R("ZN"), 0.0)
+    line(R("IOT"), io, SMALL, SMALL)
+    line(col(CN), col(C16), 1.0, 1.0)
+    ts(R("FT1"), R("FT0"), col(CN), A.is_equal, -2.0 ** -24, A.mult)
     line(R("FT"), R("FT1"), 1.0, 1.0)
+    mset(R("FT", 0, 160, 16), 0.0)
     line(R("DM"), R("M16"), 1.0e29, FAR)
     line(R("LM", 0, 160, 16), upto(10), 32.0, col(CM))
     line(R("LM", 160, 320, 16), upto(10), 32.0, col(CT))
@@ -368,7 +400,10 @@ def rank_program(g, core, T, topo):
             first = min(64 * b, 64 * hi - 128)
             mm(bk, 128, "QS" + kind, "SS" + kind, 128 * b, "QV" + kind, "SV" + kind, first)
             o = 512 * bk + 64 * b - first
-            move(R("Z" + kind, 64 * b, 64 * b + 64), R("PS", o, o + 64))
+            if kind == "n":
+                tt(R("Zn", 64 * b, 64 * b + 64), R("PS", o, o + 64), R("M64"), A.mult)
+            else:
+                line(R("Z" + kind, 64 * b, 64 * b + 64), R("PS", o, o + 64), 1.0, TINY)
 
     def blocks(k, kind, e0):
         for b in range(PIECES[k][0] // 32, PIECES[k][1] // 32):
@@ -398,16 +433,18 @@ def rank_program(g, core, T, topo):
     def sizes(k, half, kind, first, other, op):
         o = 160 * half
         a, b = PIECES[k]
-        zm, zs, eb, gt = [R(n, o + a, o + b) for n in ("ZM", "ZS", "EB", "GT")]
+        zm, gt = [R(n, o + a, o + b) for n in ("ZM", "GT")]
+        zs, eb = [R(n, o + a + 8, o + b + 8) for n in ("ZS", "EB")]
         tt(zm, diagonal(k, kind, first), R(other, a, b), op)
         tr(gt, zm)
-        scan(R("GS", o + a, o + b), R("RT", a, b), gt, 1.0, A.min, A.max)
-        scan(zs, R("RT", a, b), zm, 1.0, A.min, A.max)
-        move(eb, ends("ZS", o, k))
+        scan(R("GS", o + a + 8, o + b + 8), R("FT", a, b), gt, 0.0, A.mult, A.max)
+        scan(R("Y", o + b + 7, o + a + 7, -1), R("RS16", a, b), R("GS", o + b + 7, o + a + 7, -1), 0.0, A.mult, A.max)
+        scan(zs, R("RS16", a, b), zm, 0.0, A.mult, A.max)
+        back = [R(n, o + b + 7, o + a + 7, -1) for n in ("EB", "ZS")]
+        either(eb, v_scan(back[0], R("RS16", a, b), back[1], 0.0, A.mult, A.max), s_act(eb, ends("ZS", o + 8, k), ACT.Copy))
         tr(row(half, a, b), eb)
         times(row(half, 160 + a, 160 + b), row(half, a, b), BELOW)
-        tt(R("Y", o + a, o + b), ends("GS", o, k), R("FT", a, b), A.mult)
-        tt(R("DC", o + a, o + b), row(half, a, b), R("Y", o + a, o + b), A.is_le)
+        tt(R("DC", o + a, o + b), row(half, a, b), R("Y", o + a + 8, o + b + 8), A.is_le)
         scan(R("DG", o + a, o + b), R("RS16", a, b), R("DC", o + a, o + b), 0.0, A.mult, A.add)
 
     def fresh(k):
@@ -424,7 +461,7 @@ def rank_program(g, core, T, topo):
         move(R("SB", W * e0 + n, W * (e0 + ns), W), R("DG", 16 * e0 + 15, 16 * (e0 + ns), 16))
         for m in range(10):
             e = e0 + m
-            g_ = R("GS", 16 * e + 15, 16 * e + 16)
+            g_ = R("Y", 16 * e + 8, 16 * e + 9)
             o = 0
             for r in ([row(0, 160, 320)] if half else []) + [row(half, 16 * m + 16, 16 * m + 160)]:
                 if m < ns:
@@ -437,7 +474,7 @@ def rank_program(g, core, T, topo):
             else:
                 h = n // 2
                 scan(R("SO", 152 * e, 152 * e + h), R("CB", 304 * e, 304 * e + h), R("CB", 304 * e + h, 304 * e + n), R("DG", 16 * e + 15, 16 * e + 16), A.add, A.add)
-        sgn, top = (1.0, 0.0) if half else (-1.0, 159.0)
+        sgn, top = (1.0, -1.0) if half else (-1.0, 160.0)
         ts(R("OFFS", e0, e0 + ns), R("ACC", e0, e0 + ns), sgn, A.mult, top, A.add)
         ts(R("OFFS", e0 + ns, e0 + 10), R("SO", 152 * (e0 + ns) + n // 2 - 1, 152 * (e0 + 10), 152), sgn, A.mult, top + sgn * (n // 2), A.add)
 
@@ -446,29 +483,31 @@ def rank_program(g, core, T, topo):
         scatter(R("ORS", 16, 176), R("OFFS", 0, 10), R("VS"))
         tr(R("TS", 0, 160), R("ORS", 16, 176))
         tr(R("TS", 160, 352), R("ORS"))
-        where = (R("TS"), lst(L_3S, 1))
-        ts(R("OS", 0, 16), where, 160.0, A.add)
+        ts(R("OS", 0, 16), (R("TS"), lst(L_3S, 1)), 160.0, A.add)
         move(R("UU", 0, 160), (R("DS", 0, 320), R("OS", 0, 10)))
         for t in range(4):
-            ts(R("OS", 16 * t + 16, 16 * t + 32), where, 4.0, A.mult, 656.0 + t, A.add)
-            move(R("XP", 320 * t, 320 * t + 160), (R("AR"), R("OS", 16 * t + 16, 16 * t + 26)))
+            src, c, d = (R("AR"), 4.0, 16.0) if rnd else (R("X", 0, 656), 2.0, 14.0)
+            ts(R("OS", 16 * t + 16, 16 * t + 26), R("OS", 0, 10), c, A.mult, d + t, A.add)
+            move(R("XP", 320 * t, 320 * t + 160), (src, R("OS", 16 * t + 16, 16 * t + 26)))
         if rnd == 2:
             scatter(R("OLW", 0, 160), R("OFFS", 0, 10), R("JR", 160, 320))
 
     def order(rnd):
         count(1, NK[rnd])
-        for p, q in ((NK[rnd], 10), (0, NK[rnd])):
-            scatter(R("ORK", 320 * rnd, 320 * rnd + 320), R("OFFS", 10 + p, 10 + q), R("OLW", 160 + 16 * p, 160 + 16 * q))
+        e = 352 * rnd
+        scatter(R("ORK", e + 16, e + 336), R("OFFS", 10, 20), R("IOT"))
         for k, (a, b) in enumerate(PIECES):
-            p, q = (0, 2 * b + 16) if k == 0 else (2 * a + 16, 320)
-            o = R("ORK", 320 * rnd + p, 320 * rnd + q)
-            ts(R("FL", p, q), o, -100.0, A.is_lt, -0.5, A.mult)
-            scan(R("CU", p, q), R("FL", p, q), R("FL", p, q), R("CU", p - 1, p) if k else 0.0, A.add, A.add)
-            scan(R("VAL", 16 + p, 16 + q), R("CU", p, q), o, 0.0, A.min, A.max)
+            p, q = (16, 2 * b + 32) if k == 0 else (2 * a + 32, 336)
+            o = R("ORK", e + p, e + q)
+            scan(R("VAL", p, q), o, o, R("VAL", p - 1, p) if k else -1.0, A.add, A.add)
             n = 2 * (b - a)
-            tr(R("TT", 448 * k, 448 * k + n), R("VAL", 16 + 2 * a, 16 + 2 * b))
-            tr(R("TT", 448 * k + 192, 448 * k + 224 + n), R("VAL", 2 * a, 32 + 2 * b))
-            ts(R("OG", 16 * k, 16 * k + 16), (R("TT", 448 * k, 448 * k + 224 + n), lst(L_3G + 2 * k, 1)), 160.0, A.add)
+            for src, f, dst in (("ORK", e, "TK"), ("VAL", 0, "TT")):
+                tr(R(dst, 448 * k, 448 * k + n), R(src, f + 16 + 2 * a, f + 16 + 2 * b))
+                tr(R(dst, 448 * k + 192, 448 * k + 224 + n), R(src, f + 2 * a, f + 32 + 2 * b))
+            off = lst(L_3G + 2 * k, 1)
+            ts(R("O4", 16 * k, 16 * k + 16), (R("TK", 448 * k, 448 * k + 224 + n), off), 1.0 / SMALL, A.mult, -2.0, A.add)
+            tt(R("O4", 32 + 16 * k, 48 + 16 * k), (R("TT", 448 * k, 448 * k + 224 + n), off), R("O4", 16 * k, 16 * k + 16), A.max)
+            ts(R("OG", 16 * k, 16 * k + 16), R("O4", 32 + 16 * k, 48 + 16 * k), 161.0, A.add)
         for k, (a, b) in enumerate(PIECES):
             og = R("OG", 16 * k, 16 * k + (b - a) // 8)
             for t in range(4):
@@ -481,13 +520,12 @@ def rank_program(g, core, T, topo):
         tr(R("TD", a, b), R("DS", 2 * a, 2 * b, 2))
         c0, c1, th = 32 * k, 32 * k + 16 * ((b - a + 63) // 64), 32 * k + (b - a) // 4
         for i, c in enumerate((0.75, 0.25)):
-            times(R("TH", c0 + i, th, 4), R("TD", a, b, 16), c)
-            times(R("TH", c0 + i + 2, th, 4), R("TH", c0 + i, th, 4), -BELOW)
+            times(R("TH", c0 + 2 * i, th, 4), R("TD", a, b, 16), c)
+        times(R("TH", c0 + 1, th, 2), R("TH", c0, th, 2), -BELOW)
         scan(R("DA", a, b), R("TD", a, b), R("DM", a, b), FAR, A.max, A.min)
-        zm, zs = R("ZM", 320 + a, 320 + b), R("ZS", 320 + a, 320 + b)
-        tt(zm, diagonal(k, "n", L_X), R("M16", a, b), A.mult)
-        scan(zs, R("RS16", a, b), zm, 0.0, A.mult, A.add)
-        tt(R("CMP", c0, c1), (R("ZS", 320, 320 + b), lst(L_N + 2 * k, (c1 - c0) // 16)), R("TH", c0, c1), A.is_ge)
+        for h in range(2):
+            scan(R("ZN", 160 * h + a, 160 * h + b), R("RS32", a, b), R("Zn", 2 * a + h, 2 * b, 2), 0.0, A.mult, A.add)
+        tt(R("CMP", c0, c1), (R("ZN"), lst(L_N + 2 * k, (c1 - c0) // 16)), R("TH", c0, c1), A.is_ge)
         scan(R("CS", c0, c1), R("RS4", c0, c1), R("CMP", c0, c1), 0.0, A.mult, A.add)
         line(R("EC", a, b), (R("CS", 0, c1), lst(L_LC + a // 16, (b - a) // 16)), -0.5, 1.0)
         tr(R("D0", 2 * a + 1, 2 * b, 2), R("EC", a, b))
@@ -498,7 +536,7 @@ def rank_program(g, core, T, topo):
         tr(R("ST", a, b), R("SD", a, b))
         scan(R("PM", a, b), R("LM", a, b), R("ST", a, b), -1000.0, A.max, A.subtract)
         for t in range(4):
-            om = R("OM", 16 * t + a // 16, 16 * t + b // 16)
+            om = R("OM", 32 * k + 8 * t, 32 * k + 8 * t + (b - a) // 16)
             ts(om, R("PM", a + 15, b, 16), 4.0, A.mult, 656.0 + t, A.add)
             move(R("M", 256 + 4 * a + t, 256 + 4 * b, 4), (R("AR", 0, 16 + 8 * b), om))
 
@@ -546,8 +584,6 @@ def rank_program(g, core, T, topo):
         products(k, "e", "d", 164, L_PS)
         sizes(k, 0, "e", L_XB, "M16", A.mult)
         fresh(k)
-    for t in range(4):
-        move(R("AR", 20 + t, 1296, 8), R("X", 16 + t, 656, 4))
     for rnd in range(3):
         sort_stayers(rnd)
         order(rnd)
@@ -561,7 +597,8 @@ def rank_program(g, core, T, topo):
                 quant("QUd", "SUd", 36 + b, 128, R("X", 144 + 4 * b, 656 + 4 * b))
                 fresh(k)
         if rnd < 2:
-            tt(R("FS"), R("DS", 1, 320, 2), R("DS", 0, 320, 2), A.is_lt)
+            scan(R("FD"), R("DS", 0, 320, 2), R("DS", 1, 320, 2), 0.0, A.max, A.subtract)
+            either(R("FS"), v_ts(R("FS"), R("FD"), 0.0, A.is_gt), s_act(R("FS"), R("FD"), ACT.Sign))
             scan(R("VS"), R("JR", 0, 160), R("FS"), -1000.0, A.max, A.add)
     for k, (a, b) in enumerate(PIECES):
         act(R("OLF", 2 * a, 2 * b), (R("OLW"), R("OG", 16 * k, 16 * k + (b - a) // 8)), ACT.Identity, bias=160.0)

import numpy as np
from concourse.mybir import dt, AluOpType, ActivationFunctionType

F, B, U16, I32, C4, U8 = "float32", "bfloat16", "uint16", "int32", "float8_e4m3fn_x4", "uint8"
STEP = [1, 2, 1]
CUT = 96
W = 306
NK = [4, 4, 4]
NS = [6, 6, 6]
TINY = 2.0 ** -100
BELOW = 1.0 - 2.0 ** -24
FAR = -1.0e25
FREE = -0.5
SMALL = 2.0 ** -40
CYC, GAT, SCA, LAG, DMA, HOP, ONCE = 0.00088, 1.56, 3.5, 0.23, 1.8, 2.2, 2.0
SPARE, TURNS, SHAKES, SEED, SLACK = 0.7, 2, 4000, 1, 0.06
TAIL = 1
LAG2, FAST, ROB = 0.16, 1.15, 0.35
PLANNED = []
LEN = []


def _sb(n, d):
    return ("sbuf", [128, n], d)


PIECES = ((0, CUT), (CUT, 160))
SCRATCH = {
    "X": _sb(1296, B), "XP": _sb(1280, B), "G": _sb(1296, B), "AR": _sb(1296, B), "M": _sb(896, B), "VT": _sb(512, B),
    "WC": _sb(512, C4), "WS": _sb(512, U8), "QW": _sb(128, C4), "SW": _sb(128, U8), "QF": _sb(416, C4), "SF": _sb(416, U8),
    "QM": _sb(768, C4), "SM": _sb(768, U8), "LC": _sb(608, C4), "LS": _sb(608, U8),
    "UU": _sb(480, F), "DS": _sb(640, F), "GS": _sb(328, F), "FD": _sb(160, F), "O4": _sb(64, F),
    "ZN": _sb(320, F), "M64": _sb(64, F), "M640": _sb(64, F), "RS32": _sb(160, B), "LI": _sb(8, I32), "LT4": _sb(8, F),
    "ZM": _sb(320, F), "ZS": _sb(328, F), "EB": _sb(328, F), "GT": _sb(320, F), "Y": _sb(328, F), "DC": _sb(320, B), "DG": _sb(320, B),
    "CB": _sb(20 * 304, B), "SO": _sb(20 * 152, B), "SB": _sb(20 * W, F), "ACC": _sb(20, F), "OFFS": _sb(20, U16),
    "ORK": _sb(1056, B), "TK": _sb(896, B), "IOT": _sb(160, B), "VAL": _sb(352, B), "TT": _sb(896, B), "OG": _sb(32, U16),
    "ORS": _sb(192, B), "TS": _sb(352, B), "OS": _sb(96, U16), "FS": _sb(160, B), "VS": _sb(160, B), "OLW": _sb(320, B), "JR": _sb(320, B),
    "TD": _sb(160, F), "DA": _sb(160, F), "TH": _sb(64, F), "CMP": _sb(64, F), "CS": _sb(64, F), "EC": _sb(160, B), "D0": _sb(320, B),
    "SD": _sb(160, B), "ST": _sb(160, B), "PM": _sb(160, B), "PT": _sb(160, B), "OM": _sb(64, U16),
    "YO": _sb(320, F), "OLF": _sb(320, F),
    "PI": _sb(8, I32), "COL": _sb(24, F), "MK": _sb(2, B), "J40": _sb(40, F), "A40": _sb(40, F), "JM": _sb(40, F), "JF": _sb(40, F),
    "LF": _sb(224, F), "LST": _sb(224, U16), "RS16": _sb(160, B), "RS4": _sb(64, B), "FT0": _sb(160, F), "FT1": _sb(160, F), "FT": _sb(160, F),
    "M16": _sb(160, F), "DM": _sb(160, F), "LM": _sb(320, B), "LT": _sb(4, F),
    "PS": ("psum", [128, 4096], F),
}
for _k in "dne":
    SCRATCH["QU" + _k] = _sb(324, C4)
    SCRATCH["SU" + _k] = _sb(324, U8)
    SCRATCH["MV" + _k] = _sb(1280, B)
    SCRATCH["QV" + _k] = _sb(320, C4)
    SCRATCH["SV" + _k] = _sb(320, U8)
    SCRATCH["QS" + _k] = _sb(640, C4)
    SCRATCH["SS" + _k] = _sb(640, U8)
    SCRATCH["Z" + _k] = _sb(320, F)
NDMA = 26
SEMAPHORES = ["cv", "cs", "cp", "cg", "sent"] + ["arr%d" % _i for _i in range(6)] + ["d%d" % _i for _i in range(NDMA)]
BANKS = ((0, 1, 2, 3), (4, 5, 6, 7))

L_PS, L_PK, L_XB, L_END = 0, 40, 80, 90
L_PA, L_PR, L_LC, L_X, L_N, L_3G, L_3S = 100, 140, 180, 190, 200, 204, 208
C16, CH, CU, C32, C4Q, CQ, CE, CNE, CX16, C64, CM, CT, CG0, CG1, CS1, CN = range(1, 17)


def plan(nodes):
    if PLANNED:
        return [(nodes[i], q) for i, q in PLANNED]
    num = len(nodes)
    deps = [[p["nr"] for p in n["deps"]] for n in nodes]
    nxt = [[p["nr"] for p in n["next"]] for n in nodes]
    opts = [[(q, c) for q, (f, c) in n["opts"].items()] for n in nodes]
    lat = [n["lat"] for n in nodes]

    def fill(rank, lean, after, early):
        first = {q: [] for q in "vspgy"}
        last = {q: [] for q in "vspgy"}
        end, start, queue = [0.0] * num, [0.0] * num, [None] * num
        for i in sorted(range(num), key=lambda i: -rank[i]):
            ready = max([end[p] + LAG for p in after[i]], default=0.0) + (0.0 if early else lat[i])
            best = None
            for q, c in opts[i]:
                a, b = first[q], last[q]
                k = len(b)
                while k and b[k - 1] > ready:
                    k -= 1
                t = ready
                while k < len(a) and t + c > a[k]:
                    t = max(t, b[k])
                    k += 1
                worth = t + c + (lean[i] if q == "v" else 0.0)
                if best is None or worth < best[0]:
                    best = (worth, t, q, c, k)
            worth, t, q, c, k = best
            first[q].insert(k, t)
            last[q].insert(k, t + c)
            start[i], end[i], queue[i] = t, t + c + (lat[i] if early else 0.0), q
        return end, start, queue

    def length(order):
        end, start, queue = order
        free = {q: 0.0 for q in "vspgy"}
        late = [0.0] * num
        for i in sorted(range(num), key=lambda i: start[i]):
            t = max([late[p] + LAG2 for p in deps[i]] + [free[queue[i]]])
            free[queue[i]] = t + FAST * (end[i] - start[i] - lat[i])
            late[i] = free[queue[i]] + lat[i]
        return (1.0 - ROB) * max(end) + ROB * max(late)

    def tighten(rank, lean):
        return fill(fill(rank, lean, deps, True)[0], lean, nxt, False)[0]

    rank = [0.0] * num
    for i in reversed(range(num)):
        rank[i] = min(c for q, c in opts[i]) + lat[i] + max([LAG + rank[s] for s in nxt[i]], default=0.0)
    lean = [SPARE * dict(o).get("v", 0.0) for o in opts]
    for _ in range(TURNS):
        rank = tighten(rank, lean)
    now = fill(rank, lean, deps, True)
    best = length(now)
    rng = np.random.RandomState(SEED)
    for step in range(SHAKES):
        t0 = rng.uniform(0.0, max(now[0]))
        t1 = t0 + (2.0, 4.0, 8.0)[step % 3]
        r, l = list(rank), list(lean)
        for i in reversed(range(num)):
            if t0 <= now[1][i] <= t1:
                r[i] += float(rng.normal(0.0, 0.25))
                if len(opts[i]) > 1 and rng.uniform() < 0.2:
                    l[i] = (-0.3, 0.0, 0.1, 0.3, 1.0)[rng.randint(5)]
            for s in nxt[i]:
                r[i] = max(r[i], r[s] + 1e-6)
        if step % 4 == 0:
            r = tighten(r, l)
        new = fill(r, l, deps, True)
        span = length(new)
        if span <= best + SLACK * (1.0 - step / SHAKES):
            rank, lean, now, best = r, l, new, span
    PLANNED.extend((i, now[2][i]) for i in sorted(range(num), key=lambda i: (now[1][i], i)))
    LEN.append(max(now[0]))
    return plan(nodes)


def rank_program(g, core, T, topo):
    rank = T.rank_of(core)
    if rank is None:
        return
    A = AluOpType
    ACT = ActivationFunctionType
    eng = {"v": g.vector, "s": g.scalar, "p": g.tensor, "g": g, "y": g.sync}
    sem = {"v": "cv", "s": "cs", "p": "cp", "g": "cg"}
    nodes = []
    hist = {}

    def R(name, a=0, b=None, s=1):
        n = SCRATCH[name][1][1]
        return (name, a, n if b is None else min(b, n), s)

    def ap(r):
        if r[3] == 1:
            return T[r[0]][:, r[1]:r[2]]
        return T[r[0]][:, r[1]:r[2]:r[3]]

    def size(r):
        return len(range(r[1], r[2], r[3]))

    def call(opts, reads, writes, kind="op", lat=0.0):
        n = {"opts": opts, "deps": [], "next": [], "kind": kind, "lat": lat, "nr": len(nodes), "w": (writes or reads)[0][0]}
        seen = set()
        sets = []
        for r, wr in [(r, r[0] == "PS") for r in reads] + [(r, True) for r in writes]:
            s = frozenset([r[1] // 512]) if r[0] == "PS" else frozenset(range(r[1], r[2], r[3]))
            sets.append((r[0], s, wr))
            for s2, wr2, m in hist.get(r[0], []):
                if (wr or wr2) and m["nr"] not in seen and not s.isdisjoint(s2):
                    seen.add(m["nr"])
                    n["deps"].append(m)
                    m["next"].append(n)
        for name, s, wr in sets:
            h = hist.setdefault(name, [])
            if wr:
                h[:] = [e for e in h if not e[0] <= s]
            h.append((s, wr, n))
        nodes.append(n)
        return n

    def opnd(x):
        if len(x) == 2:
            return ap(x[0]).indirect(ap(x[1])), [x[0], x[1]]
        return ap(x), [x]

    def scal(x):
        if isinstance(x, tuple):
            return ap(x), [x]
        return x, []

    def cost(out, in0, per, others=()):
        if len(in0) == 2:
            return 0.06 + GAT * CYC * size(out)
        if per is None:
            per = 0.5 if all(SCRATCH[r[0]][2] in (B, U16) for r in [out, in0] + list(others)) else 1.0
        return CYC * max(64, per * size(out))

    def col(c):
        return R("COL", c, c + 1)

    def lst(c, n):
        return R("LST", c, c + n)

    def v_ts(out, in0, s1, op0, s2=None, op1=None):
        i, rd = opnd(in0)
        a1, r1 = scal(s1)
        a2, r2 = scal(s2)
        c = cost(out, in0, None, r1 + r2)
        if op1 is None:
            return (lambda e: e.tensor_scalar(ap(out), i, a1, None, op0), c), rd + r1
        return (lambda e: e.tensor_scalar(ap(out), i, a1, a2, op0, op1), c), rd + r1 + r2

    def s_act(out, in_, func, bias=None, scale=None, accum=None):
        i, rd = opnd(in_)
        kw = {}
        if bias is not None:
            kw["bias"], r = scal(bias)
            rd = rd + r
        if scale is not None:
            kw["scale"], r = scal(scale)
            rd = rd + r
        if accum is not None:
            kw["accum_out"] = ap(accum)
        return (lambda e: e.activation(ap(out), i, func, **kw), cost(out, in_, 1.0) + (0.02 if accum else 0.0)), rd

    def ts(out, in0, s1, op0, s2=None, op1=None):
        o, rd = v_ts(out, in0, s1, op0, s2, op1)
        return call({"v": o}, rd, [out])

    def act(out, in_, func, bias=None, scale=None, accum=None):
        o, rd = s_act(out, in_, func, bias, scale, accum)
        return call({"s": o}, rd, [out] + ([accum] if accum else []))

    def either(out, v, s):
        return call({"v": v[0], "s": s[0]}, v[1] + s[1], [out])

    def v_cp(out, in_):
        i, rd = opnd(in_)
        return (lambda e: e.tensor_copy(ap(out), i), cost(out, in_, None)), rd

    def cp(out, in_):
        o, rd = v_cp(out, in_)
        return call({"v": o}, rd, [out])

    def move(out, in_):
        return either(out, v_cp(out, in_), s_act(out, in_, ACT.Copy))

    def times(out, in_, c):
        return either(out, v_ts(out, in_, c, A.mult), s_act(out, in_, ACT.Copy, scale=c))

    def line(out, in_, c, d):
        return either(out, v_ts(out, in_, c, A.mult, d, A.add), s_act(out, in_, ACT.Identity, bias=d, scale=c))

    def mask(out, in_, h):
        return either(out, v_ts(out, in_, R("MK", h, h + 1), A.mult), s_act(out, in_, ACT.Copy, scale=col(CH if h else CE)))

    def tt(out, in0, in1, op):
        i, rd = opnd(in0)
        return call({"v": (lambda e: e.tensor_tensor(ap(out), i, ap(in1), op), cost(out, in0, 1.0 if in0[0] == "PS" else 2.0))}, rd + [in1], [out])

    def v_scan(out, d0, d1, init, op0, op1):
        a, r = scal(init)
        return (lambda e: e.tensor_tensor_scan(ap(out), ap(d0), ap(d1), a, op0, op1), cost(out, d0, None, [d1] + r)), [d0, d1] + r

    def scan(out, d0, d1, init, op0, op1):
        o, rd = v_scan(out, d0, d1, init, op0, op1)
        return call({"v": o}, rd, [out])

    def tr(out, in_):
        return call({"v": (lambda e: e.transpose(ap(out), ap(in_)), cost(out, in_, None))}, [in_], [out])

    def g_iota(out, pat, base, cm=0):
        c = 0.14 + 2 * CYC * size(out) + LAG
        if SCRATCH[out[0]][2] == I32:
            return (lambda e: e.iota(ap(out), pat, base, cm), c)
        return (lambda e: e.iota(ap(out), pat, base, cm, allow_small_or_imprecise_dtypes=True), c)

    def iota(out, pat, base, cm=0):
        return call({"g": g_iota(out, pat, base, cm)}, [], [out])

    def mset(out, val, plain=False):
        opts = {"v": (lambda e: e.memset(ap(out), val), cost(out, out, None))}
        if val == int(val) and abs(val) <= 1000 and not plain:
            opts["g"] = g_iota(out, [[0, size(out)]], int(val))
        return call(opts, [], [out])

    def scatter(win, off, src):
        return call({"v": (lambda e: e.tensor_copy(ap(win).indirect(ap(off)), ap(src)), 0.06 + SCA * CYC * size(src))}, [off, src], [win])

    def quant(qc, qs, a, n, tile):
        oc, os_ = R(qc, a, a + n), R(qs, a, a + n)
        return call({"v": (lambda e: e.quantize_mx(ap(oc), ap(os_), ap(tile)), 0.013 + 0.00097 * n)}, [tile], [oc, os_])

    def mm(bk, n, lc, ls, la, rc, rs, ra):
        o = R("PS", 512 * bk, 512 * bk + n)
        rr = [R(lc, la, la + 128), R(ls, la, la + 128), R(rc, ra, ra + n), R(rs, ra, ra + n)]
        return call({"p": (lambda e: e.matmul_mx(ap(o), ap(rr[0]), ap(rr[1]), ap(rr[2]), ap(rr[3]), True, True), 0.0007 * (n + 16))}, rr, [o])

    def dma(qs, out, in_, reads, writes):
        return call({q: (lambda e: e.dma_start(out, in_), 0.1) for q in qs}, reads, writes, "dma", DMA)

    dma("y", T.X[:, 16:656], T.x[:, 0:640], [], [R("X", 16, 656)])
    dma("y", T.X[:, 656:1296], T.x[:, 640:1280], [], [R("X", 656, 1296)])
    dma("y", T.WC[:].bitcast(dt.uint8), T.wc[:], [], [R("WC")])
    dma("y", T.WS[:], T.ws[:], [], [R("WS")])
    dma("y", T.VT[:], T.v[:], [], [R("VT")])

    io = R("OLW", 160, 320)

    def upto(n):
        return R("OLW", 160, 160 + n)

    def lf(c, n, s=1):
        return R("LF", c, c + n, s)

    iota(R("PI", 0, 1), [[0, 1]], 0, 1)
    iota(R("J40"), [[32, 5], [0, 4], [16, 2]], 1000)
    iota(R("A40"), [[0, 5], [1, 4], [0, 2]], 0)
    iota(R("FT0"), [[0, 10], [1, 16]], 0)
    iota(io, [[1, 160]], 0)
    for name in ("X", "G", "AR"):
        mset(R(name, 0, 16), 0.0, True)
    mset(R("M", 4 * CUT - 256, 256), 0.0, True)
    for r, val in ((R("RS16"), 1.0), (R("RS16", 0, 160, 16), 0.0), (R("RS4"), 1.0), (R("RS4", 0, 64, 4), 0.0),
                   (R("VAL"), 0.0), (R("ORS"), 0.0), (R("D0"), 0.0), (R("TH"), 0.0), (R("LM"), -1000.0), (lf(L_N, 24), 0.0),
                   (R("ORK", 0, 352), FREE), (R("ORK", 352, 704), FREE), (R("ORK", 704, 1056), FREE)):
        mset(r, val)
    p0 = R("PI", 0, 1)
    ts(R("PI", C16, C16 + 1), p0, 15, A.bitwise_and)
    ts(R("PI", CH, CH + 1), p0, 4, A.logical_shift_right, 1, A.bitwise_and)
    ts(R("PI", CU, CU + 1), p0, 1, A.bitwise_and)
    ts(R("PI", C32, C32 + 1), p0, 31, A.bitwise_and)
    ts(R("PI", C4Q, C4Q + 1), p0, 2, A.logical_shift_right, 3, A.bitwise_and)
    ts(R("PI", CQ, CQ + 1), p0, 5, A.logical_shift_right)
    cp(R("COL", 1, 7), R("PI", 1, 7))
    line(R("MK", 0, 1), col(CH), -1.0, 1.0)
    move(R("MK", 1, 2), col(CH))
    line(col(CE), col(CH), -1.0, 1.0)
    tt(col(CNE), col(CU), col(CH), A.not_equal)
    times(col(CX16), col(C16), 16.0)
    times(col(C64), col(C32), 2.0)
    line(col(CM), col(C16), 2.0, -159.0)
    line(col(CT), col(C16), 2.0, -160.0)
    ts(R("JM"), R("A40"), col(CQ), A.is_equal)
    line(R("J40"), R("J40"), 1.0, col(C16))
    tt(R("JF"), R("J40"), R("JM"), A.mult)
    for first, c, d in ((L_PS, 1.0, -996.0), (L_PK, 1.0, -836.0), (L_PA, 2.0, -1996.0), (L_PR, 2.0, -1995.0)):
        act(lf(first, 40), R("JF"), ACT.Relu, bias=d, scale=c)
    line(lf(L_XB, 10), upto(10), 32.0, col(C32))
    line(lf(L_END, 10), upto(10), 16.0, 15.0)
    cp(lst(0, L_PA), lf(0, L_PA))
    line(lf(L_X, 10, 2), upto(5), 64.0, col(C64))
    line(lf(L_X + 1, 9, 2), lf(L_X, 10, 2), 1.0, 1.0)
    line(R("LT"), upto(4), 4.0, col(C4Q))
    for k, (a, b) in enumerate(PIECES):
        line(lf(L_LC + a // 16, (b - a) // 16), upto((b - a) // 16), 4.0, 3.0 + 32.0 * k)
        ts(R("JM", 2 * k, 2 * k + 2), R("LT", 0, 2), (b - a) / 16.0 - 1.0, A.min)
        cp(R("LI", 2 * k, 2 * k + 2), R("JM", 2 * k, 2 * k + 2))
        ts(R("LI", 4 + 2 * k, 6 + 2 * k), R("LI", 2 * k, 2 * k + 2), 1, A.bitwise_and)
        cp(R("LT4", 2 * k, 2 * k + 2), R("LI", 4 + 2 * k, 6 + 2 * k))
        line(R("LT4", 4 + 2 * k, 6 + 2 * k), R("JM", 2 * k, 2 * k + 2), 16.0, 31.0 + a)
        times(R("LT4", 2 * k, 2 * k + 2), R("LT4", 2 * k, 2 * k + 2), 144.0)
        tt(lf(L_N + 2 * k, 2), R("LT4", 2 * k, 2 * k + 2), R("LT4", 4 + 2 * k, 6 + 2 * k), A.add)
    for first, c, top, far in ((L_3G, CG0, 11.0, 208.0), (L_3G + 2, CG1, 7.0, 208.0), (L_3S, CS1, 9.0, 176.0)):
        ts(col(c), col(C16), top, A.min, 16.0, A.mult)
        line(lf(first, 1), col(CNE), far, col(c))
    cp(lst(L_PA, 124), lf(L_PA, 124))
    ts(R("M16"), R("FT0"), col(C16), A.is_equal)
    iota(R("M640"), [[1, 32], [0, 2]], 0)
    ts(R("M64"), R("M640"), col(C32), A.is_equal)
    mset(R("RS32"), 1.0)
    mset(R("RS32", 0, 160, 32), 0.0)
    mset(R("ZN"), 0.0)
    line(R("IOT"), io, SMALL, SMALL)
    line(col(CN), col(C16), 1.0, 1.0)
    ts(R("FT1"), R("FT0"), col(CN), A.is_equal, -2.0 ** -24, A.mult)
    line(R("FT"), R("FT1"), 1.0, 1.0)
    mset(R("FT", 0, 160, 16), 0.0)
    line(R("DM"), R("M16"), 1.0e29, FAR)
    line(R("LM", 0, 160, 16), upto(10), 32.0, col(CM))
    line(R("LM", 160, 320, 16), upto(10), 32.0, col(CT))
    line(R("VS"), io, 2.0, -159.0)
    line(R("JR", 0, 160), io, 2.0, -160.0)
    line(R("JR", 160, 320), io, 1.0, -160.0)

    def products(k, kind, qu, n, plist):
        lo, hi = PIECES[k][0] // 32, PIECES[k][1] // 32
        quant("QV" + kind, "SV" + kind, 64 * lo, 64 * (hi - lo), R("MV" + kind, 256 * lo, 256 * hi))
        off = lst(plist + 8 * lo, 8 * (hi - lo))
        oc, os_ = R("QS" + kind, 128 * lo, 128 * hi), R("SS" + kind, 128 * lo, 128 * hi)
        wc, ws = R("QU" + qu, 0, n), R("SU" + qu, 0, n)
        move(os_, (ws, off))
        call({"v": (lambda e: e.tensor_copy(ap(oc).bitcast(dt.uint32), ap(wc).bitcast(dt.uint32).indirect(ap(off))), cost(oc, (wc, off), None))}, [wc, off], [oc])
        for b in range(lo, hi):
            bk = BANKS[k][b - lo + ("n" == kind)]
            first = min(64 * b, 64 * hi - 128)
            mm(bk, 128, "QS" + kind, "SS" + kind, 128 * b, "QV" + kind, "SV" + kind, first)
            o = 512 * bk + 64 * b - first
            if kind == "n":
                tt(R("Zn", 64 * b, 64 * b + 64), R("PS", o, o + 64), R("M64"), A.mult)
            else:
                line(R("Z" + kind, 64 * b, 64 * b + 64), R("PS", o, o + 64), 1.0, TINY)

    def blocks(k, kind, e0):
        for b in range(PIECES[k][0] // 32, PIECES[k][1] // 32):
            for h in range(2):
                mask(R("MV" + kind, 256 * b + 128 * h, 256 * b + 128 * h + 128), R("X", e0 + 128 * b, e0 + 128 * b + 128), h)

    def pairs(k, kind, src, plist):
        a, b = PIECES[k]
        first = 0 if k == 0 else 4 + 2 * a
        quant("QU" + kind, "SU" + kind, first, 4 + 2 * b - first, R(src, 4 * first, 16 + 8 * b))
        for h in range(2):
            for t in range(4):
                mask(R("MV" + kind, 8 * a + 4 * h + t, 8 * b, 8), R(src, 20 + 8 * a + t, 16 + 8 * b, 8), h)
        products(k, kind, kind, 4 + 2 * b, plist)

    def diagonal(k, kind, first):
        a, b = PIECES[k]
        return (R("Z" + kind, 0, 2 * b), lst(first + a // 16, (b - a) // 16))

    def ends(buf, o, k):
        a, b = PIECES[k]
        return (R(buf, o, o + b), lst(L_END + a // 16, (b - a) // 16))

    def row(half, a, b):
        return R("DS", 2 * a + 1, 2 * b + 1, 2) if half == 0 else R("UU", 160 + a, 160 + b)

    def sizes(k, half, kind, first, other, op):
        o = 160 * half
        a, b = PIECES[k]
        zm, gt = [R(n, o + a, o + b) for n in ("ZM", "GT")]
        zs, eb = [R(n, o + a + 8, o + b + 8) for n in ("ZS", "EB")]
        tt(zm, diagonal(k, kind, first), R(other, a, b), op)
        tr(gt, zm)
        scan(R("GS", o + a + 8, o + b + 8), R("FT", a, b), gt, 0.0, A.mult, A.max)
        scan(R("Y", o + b + 7, o + a + 7, -1), R("RS16", a, b), R("GS", o + b + 7, o + a + 7, -1), 0.0, A.mult, A.max)
        scan(zs, R("RS16", a, b), zm, 0.0, A.mult, A.max)
        back = [R(n, o + b + 7, o + a + 7, -1) for n in ("EB", "ZS")]
        either(eb, v_scan(back[0], R("RS16", a, b), back[1], 0.0, A.mult, A.max), s_act(eb, ends("ZS", o + 8, k), ACT.Copy))
        tr(row(half, a, b), eb)
        times(row(half, 160 + a, 160 + b), row(half, a, b), BELOW)
        tt(R("DC", o + a, o + b), row(half, a, b), R("Y", o + a + 8, o + b + 8), A.is_le)
        scan(R("DG", o + a, o + b), R("RS16", a, b), R("DC", o + a, o + b), 0.0, A.mult, A.add)

    def fresh(k):
        a, b = PIECES[k]
        blocks(k, "d", 656)
        products(k, "d", "d", 164 + b, L_PK)
        for t in range(4):
            move(R("XP", 320 * t + 160 + a, 320 * t + 160 + b), R("X", 656 + 4 * a + t, 656 + 4 * b, 4))
        sizes(k, 1, "d", L_XB, "M16", A.mult)

    def count(half, ns):
        e0 = 10 * half
        n = 144 + 160 * half
        move(R("SB", W * e0 + n, W * (e0 + ns), W), R("DG", 16 * e0 + 15, 16 * (e0 + ns), 16))
        for m in range(10):
            e = e0 + m
            g_ = R("Y", 16 * e + 8, 16 * e + 9)
            o = 0
            for r in ([row(0, 160, 320)] if half else []) + [row(half, 16 * m + 16, 16 * m + 160)]:
                if m < ns:
                    act(R("SB", W * e + o, W * e + o + size(r)), r, ACT.Sign, bias=g_, scale=-1.0)
                else:
                    ts(R("CB", 304 * e + o, 304 * e + o + size(r)), r, g_, A.is_lt, 0.5, A.subtract)
                o += size(r)
            if m < ns:
                act(R("SB", W * e, W * e + n + 1), R("SB", W * e, W * e + n + 1), ACT.Relu, accum=R("ACC", e, e + 1))
            else:
                h = n // 2
                scan(R("SO", 152 * e, 152 * e + h), R("CB", 304 * e, 304 * e + h), R("CB", 304 * e + h, 304 * e + n), R("DG", 16 * e + 15, 16 * e + 16), A.add, A.add)
        sgn, top = (1.0, -1.0) if half else (-1.0, 160.0)
        ts(R("OFFS", e0, e0 + ns), R("ACC", e0, e0 + ns), sgn, A.mult, top, A.add)
        ts(R("OFFS", e0 + ns, e0 + 10), R("SO", 152 * (e0 + ns) + n // 2 - 1, 152 * (e0 + 10), 152), sgn, A.mult, top + sgn * (n // 2), A.add)

    def sort_stayers(rnd):
        count(0, NS[rnd])
        scatter(R("ORS", 16, 176), R("OFFS", 0, 10), R("VS"))
        tr(R("TS", 0, 160), R("ORS", 16, 176))
        tr(R("TS", 160, 352), R("ORS"))
        ts(R("OS", 0, 16), (R("TS"), lst(L_3S, 1)), 160.0, A.add)
        move(R("UU", 0, 160), (R("DS", 0, 320), R("OS", 0, 10)))
        for t in range(4):
            src, c, d = (R("AR"), 4.0, 16.0) if rnd else (R("X", 0, 656), 2.0, 14.0)
            ts(R("OS", 16 * t + 16, 16 * t + 26), R("OS", 0, 10), c, A.mult, d + t, A.add)
            move(R("XP", 320 * t, 320 * t + 160), (src, R("OS", 16 * t + 16, 16 * t + 26)))
        if rnd == 2:
            scatter(R("OLW", 0, 160), R("OFFS", 0, 10), R("JR", 160, 320))

    def order(rnd):
        count(1, NK[rnd])
        e = 352 * rnd
        scatter(R("ORK", e + 16, e + 336), R("OFFS", 10, 20), R("IOT"))
        for k, (a, b) in enumerate(PIECES):
            p, q = (16, 2 * b + 32) if k == 0 else (2 * a + 32, 336)
            o = R("ORK", e + p, e + q)
            scan(R("VAL", p, q), o, o, R("VAL", p - 1, p) if k else -1.0, A.add, A.add)
            n = 2 * (b - a)
            for src, f, dst in (("ORK", e, "TK"), ("VAL", 0, "TT")):
                tr(R(dst, 448 * k, 448 * k + n), R(src, f + 16 + 2 * a, f + 16 + 2 * b))
                tr(R(dst, 448 * k + 192, 448 * k + 224 + n), R(src, f + 2 * a, f + 32 + 2 * b))
            off = lst(L_3G + 2 * k, 1)
            ts(R("O4", 16 * k, 16 * k + 16), (R("TK", 448 * k, 448 * k + 224 + n), off), 1.0 / SMALL, A.mult, -2.0, A.add)
            tt(R("O4", 32 + 16 * k, 48 + 16 * k), (R("TT", 448 * k, 448 * k + 224 + n), off), R("O4", 16 * k, 16 * k + 16), A.max)
            ts(R("OG", 16 * k, 16 * k + 16), R("O4", 32 + 16 * k, 48 + 16 * k), 161.0, A.add)
        for k, (a, b) in enumerate(PIECES):
            og = R("OG", 16 * k, 16 * k + (b - a) // 8)
            for t in range(4):
                move(R("G", 16 + 8 * a + t, 16 + 8 * b, 4), (R("XP", 320 * t, 320 * t + 320), og))
            move(R("DS", 2 * a, 2 * b), (R("UU", 0, 320), og))

    def reduce(k):
        a, b = PIECES[k]
        pairs(k, "n", "G", L_PA)
        tr(R("TD", a, b), R("DS", 2 * a, 2 * b, 2))
        c0, c1, th = 32 * k, 32 * k + 16 * ((b - a + 63) // 64), 32 * k + (b - a) // 4
        for i, c in enumerate((0.75, 0.25)):
            times(R("TH", c0 + 2 * i, th, 4), R("TD", a, b, 16), c)
        times(R("TH", c0 + 1, th, 2), R("TH", c0, th, 2), -BELOW)
        scan(R("DA", a, b), R("TD", a, b), R("DM", a, b), FAR, A.max, A.min)
        for h in range(2):
            scan(R("ZN", 160 * h + a, 160 * h + b), R("RS32", a, b), R("Zn", 2 * a + h, 2 * b, 2), 0.0, A.mult, A.add)
        tt(R("CMP", c0, c1), (R("ZN"), lst(L_N + 2 * k, (c1 - c0) // 16)), R("TH", c0, c1), A.is_ge)
        scan(R("CS", c0, c1), R("RS4", c0, c1), R("CMP", c0, c1), 0.0, A.mult, A.add)
        line(R("EC", a, b), (R("CS", 0, c1), lst(L_LC + a // 16, (b - a) // 16)), -0.5, 1.0)
        tr(R("D0", 2 * a + 1, 2 * b, 2), R("EC", a, b))
        for t in range(4):
            scan(R("AR", 16 + 8 * a + t, 16 + 8 * b, 4), R("D0", 2 * a, 2 * b), R("G", 16 + 8 * a + t, 16 + 8 * b, 4), 0.0, A.mult, A.add)
        pairs(k, "e", "AR", L_PR)
        tt(R("SD", a, b), diagonal(k, "e", L_X), R("DA", a, b), A.is_lt)
        tr(R("ST", a, b), R("SD", a, b))
        scan(R("PM", a, b), R("LM", a, b), R("ST", a, b), -1000.0, A.max, A.subtract)
        for t in range(4):
            om = R("OM", 32 * k + 8 * t, 32 * k + 8 * t + (b - a) // 16)
            ts(om, R("PM", a + 15, b, 16), 4.0, A.mult, 656.0 + t, A.add)
            move(R("M", 256 + 4 * a + t, 256 + 4 * b, 4), (R("AR", 0, 16 + 8 * b), om))

    nsent = [0]

    def hand_on(rnd, k):
        a, b = PIECES[k]
        n, o, to = b - a, 256 * rnd + 128 * k + 128, 128 + 160 * rnd + a
        quant("QM", "SM", o - 128, 128, R("M", 4 * b - 256, 4 * b + 256))
        dst = T.cores[(rank + STEP[rnd]) % len(T.cores)]
        src = T.cores[(rank - STEP[rnd]) % len(T.cores)]
        arr = "arr%d" % (2 * rnd + k)

        def calls(e):
            rid, pid, _ = topo.addr(dst)
            engines = topo.mask(core, dst)
            e.remote_dma(T.LC[:, to:to + n].bitcast(dt.uint8), T.QM[:, o - n:o].bitcast(dt.uint8), T.sem[arr], T.sem.sent, pid, rid, engines)
            e.remote_dma(T.LS[:, to:to + n], T.SM[:, o - n:o], T.sem[arr], T.sem.sent, pid, rid, engines)
            nsent[0] += 2 * len(topo.engines(core, dst))
        node = call({"g": (calls, 0.6 + ONCE * (rnd + k == 0))}, [R("QM", o - n, o), R("SM", o - n, o)], [R("LC", to, to + n), R("LS", to, to + n)], "remote", HOP)
        node["tok"] = (arr, 2 * len(topo.engines(src, core)), {})

    def layer(rnd, k):
        a, b = PIECES[k]
        for i in range(4):
            bk = BANKS[k][i]
            mm(bk, 128, "WC", "WS", 128 * i, "LC", "LS", 160 * rnd + b)
            times(R("X", 656 + 4 * a + i, 656 + 4 * b, 4), R("PS", 512 * bk + 128 - (b - a), 512 * bk + 128), 0.03125)

    def finish(a, b, o, bk):
        n, m = b - a, max(b - a, 128)
        quant("QF", "SF", o - m, m, R("X", 16 + 4 * (b - m), 16 + 4 * b))
        mm(bk, m, "QW", "SW", 0, "QF", "SF", o - m)
        dma("ys", T.oc[:, 4 * a:4 * b], T.QF[:, o - n:o].bitcast(dt.uint8), [R("QF", o - n, o)], [])
        for k in range(4):
            dma("ys", T.osc[4 * k:4 * k + 4, a:b], T.SF[32 * k:32 * k + 4, o - n:o], [R("SF", o - n, o)], [])
        move(R("YO", a, b), R("PS", 512 * bk + m - n, 512 * bk + m))
        dma("ys", T.y[:, a:b], T.YO[:, a:b], [R("YO", a, b)], [])

    quant("QUd", "SUd", 0, 164, R("X", 0, 656))
    quant("QUd", "SUd", 164, 160, R("X", 656, 1296))
    quant("LC", "LS", 0, 128, R("X", 0, 512))
    for k in range(2):
        blocks(k, "e", 16)
        products(k, "e", "d", 164, L_PS)
        sizes(k, 0, "e", L_XB, "M16", A.mult)
        fresh(k)
    for rnd in range(3):
        sort_stayers(rnd)
        order(rnd)
        for k, (a, b) in enumerate(PIECES):
            reduce(k)
            hand_on(rnd, k)
            if rnd < 2:
                sizes(k, 0, "e", L_X, "DA", A.min)
            layer(rnd, k)
            if rnd < 2:
                quant("QUd", "SUd", 36 + b, 128, R("X", 144 + 4 * b, 656 + 4 * b))
                fresh(k)
        if rnd < 2:
            scan(R("FD"), R("DS", 0, 320, 2), R("DS", 1, 320, 2), 0.0, A.max, A.subtract)
            either(R("FS"), v_ts(R("FS"), R("FD"), 0.0, A.is_gt), s_act(R("FS"), R("FD"), ACT.Sign))
            scan(R("VS"), R("JR", 0, 160), R("FS"), -1000.0, A.max, A.add)
    for k, (a, b) in enumerate(PIECES):
        act(R("OLF", 2 * a, 2 * b), (R("OLW"), R("OG", 16 * k, 16 * k + (b - a) // 8)), ACT.Identity, bias=160.0)
    dma("y", T.ol[:], T.OLF[0:128:16, :], [R("OLF")], [])
    scan(R("PT"), R("LM", 160, 320), R("ST"), -1000.0, A.max, A.add)
    for t in range(4):
        ts(R("OS", 16 * t + 16, 16 * t + 26), R("PT", 15, 160, 16), 4.0, A.mult, 656.0 + t, A.add)
        move(R("X", 16 + t, 656, 4), (R("AR"), R("OS", 16 * t + 16, 16 * t + 26)))
    quant("QW", "SW", 0, 128, R("VT"))
    finish(0, 160, 160, 0)
    if TAIL:
        finish(160, 160 + CUT, 288, 1)
        finish(160 + CUT, 320, 416, 4)
    else:
        finish(160, 320, 320, 1)

    done = {q: 0 for q in sem}
    known = {q: {} for q in eng}
    ndma = 0

    def wait(q, tok):
        if known[q].get(tok[0], 0) < tok[1]:
            eng[q].wait_ge(T.sem[tok[0]], tok[1])
            known[q][tok[0]] = tok[1]
            for k, val in tok[2].items():
                if known[q].get(k, 0) < val:
                    known[q][k] = val

    for n, q in plan(nodes):
        need = {}
        for p in n["deps"]:
            tok = p["tok"]
            if tok[0] not in need or need[tok[0]][1] < tok[1]:
                need[tok[0]] = tok
        for tok in sorted(need.values(), key=lambda tok: -len(tok[2])):
            wait(q, tok)
        if q == "g":
            wait("g", ("cg", done["g"], {}))
        ins = n["opts"][q][0](eng[q])
        clock = dict(known[q])
        if n["kind"] == "dma":
            name = "d%d" % ndma
            ndma += 1
            ins.then_inc(T.sem[name], 16)
            n["tok"] = (name, 16, clock)
        elif n["kind"] == "op":
            done[q] += 1
            ins.then_inc(T.sem[sem[q]], 1)
            n["tok"] = (sem[q], done[q], clock)

    g.wait_ge(T.sem.sent, nsent[0])
    for q in ("v", "s", "p", "g"):
        g.wait_ge(T.sem[sem[q]], done[q])
    for i in range(ndma):
        g.wait_ge(T.sem["d%d" % i], 16)
